import numpy as np, ml_dtypes
CORES = [113,118,241,246]
N = 4
BF = ml_dtypes.bfloat16
def gentries(a):
    return np.ascontiguousarray(a.reshape(8, 16, -1).transpose(0, 2, 1)).reshape(8, -1)
def gtable(e):
    e = np.asarray(e); return np.ascontiguousarray(e.reshape(8, -1, 16).transpose(0, 2, 1)).reshape(128, -1).astype(np.int32)
V, E, G, P, K, J, RO, CM = 1024, 2048, 256, 2816, 4, 6, 4, 63
NEED = 9
NV = (9, 8, 16, 15, 0, 9, 8, 7)
NI = 2 * (K - 1) + 2 * (N - 1) * K
def cover(rng):
    return ((CM + 1) * (0.5 * rng.random((1, V)) + 0.5 * rng.random((16, V)))).astype(np.int64)
def blank():
    return np.full((K, E), -1), np.ones((K, P), bool)
def put(L, free, i, e, t):
    if L[i, e] < 0 and free[i, t]:
        L[i, e] = t; free[i, t] = False
def pair(L, free, c, l, e, f, up=0, down=0):
    i = (c[e] + l) % K; j = (c[f] + l) % K
    ok = (L[i, e] < 0) & (L[j, f] < 0) & free[i, f + up] & free[j, e + down]
    i, j, e, f = i[ok], j[ok], e[ok], f[ok]
    L[i, e] = f + up; L[j, f] = e + down; free[i, f + up] = False; free[j, e + down] = False
def sides(rng, reads):
    s = rng.integers(0, 2, len(reads)); return 2 * reads + s, 2 * reads + 1 - s
def weave(rng, L, free, c, reads, q):
    a, b = sides(rng, reads); b = np.roll(b, -1); keep = rng.random(len(reads)) >= q; more = keep & (rng.random(len(reads)) < 0.33)
    pair(L, free, c, 0, a[keep], b[keep]); pair(L, free, c, 1, a[more], b[more])
    u = np.concatenate([a[~keep], b[~keep]])
    v = rng.permutation(u[(u < (N - 1) * G) & (u % G < G - 8)])[:8]; k = len(v) // 4
    pair(L, free, c, 0, v[:k], v[k:2 * k], E, E); pair(L, free, c, 0, v[2 * k:3 * k], v[3 * k:4 * k], E, 0)
    for l in range(1, RO):
        u = rng.permutation(u); k = 3 * len(u) // 10; pair(L, free, c, l, u[:k], u[k:2 * k]); u = u[2 * k:]
def fill(rng, L, free, shut):
    free[:, shut] = False
    for i in range(K):
        e = np.flatnonzero(L[i] < 0); L[i, e] = rng.permutation(np.flatnonzero(free[i]))[:len(e)]
def closed(reads, k):
    reads = np.asarray(reads, np.int64)
    return np.concatenate([2 * reads, 2 * reads + 1] + [E + d * G + G - 1 - np.arange(k) for d in range(N - 1)]).astype(np.int64)
def show(rng, pool, last):
    return np.concatenate([rng.permutation(pool)[:G - len(last)], np.array(last, np.int64)])
def join(rng, L, free, c, reads, k):
    s = rng.integers(0, 2, len(reads)); s[k - 1] = reads[k - 1] & 1
    o, n = 2 * reads + s, 2 * reads + 1 - s; pair(L, free, c, 0, o[:-1], n[1:]); return o, n
def duel(rng, L, free, c, X, Y, Z, t, s):
    o, n = join(rng, L, free, c, np.concatenate([X, Y]), len(X)); f, b = int(o[len(X) - 1]), int(n[len(X)])
    o, n = join(rng, L, free, c, Z, len(Z)); e, h = int(o[-1]), int(n[0])
    if (c[e] + t - c[b]) % K == 0: c[e] = K - 1 - c[e]
    for l in range(t, RO): put(L, free, (c[e] + l) % K, e, f)
    for l in range(s, RO): put(L, free, (c[h] + l) % K, h, E + ((N - 2 + l - s) % (N - 1)) * G + G - 1)
    return f, e
def paint(rng, x, X, Y, Z, nv, inv, near):
    hi, lo = (0, CM) if inv else (CM, 0); on = rng.permutation(16)[:nv]
    x[:, X] = hi; x[:, Y] = lo; x[:, Z] = lo
    if near: x[on, Z[-1]] = CM - 1 if inv else 1
    else: x[np.ix_(on, Z)] = hi
def edge(me, mf, mh, d):
    wf = next(w for w in range(CM * mf // 2, 0, -1) if (2 * w * mh * me - d) % mf == 0); s = (2 * wf * mh * me - d) // mf
    we = next(w for w in range(s // mh, 0, -1) if (s - w * mh) % me == 0)
    return we, wf, (s - we * mh) // me
def fine(rng, L, free, c, x, X, Y, Z, t, nv, inv):
    duel(rng, L, free, c, X, Y, Z, t, RO)
    p = np.concatenate([rng.permutation(np.array([0, 1, 14, 15])), 2 + rng.permutation(12)])
    if nv < NEED: p = p[::-1]
    for j in range(16):
        for q, s in zip((Z, X, Y), edge(len(Z), len(X), len(Y), 1 if j < nv else -(j % 2))):
            v = s // len(q) + (np.arange(len(q)) < s % len(q)); x[p[j], q] = CM - v if inv else v
def draw(rng, one):
    t = [[one(rng, r, g) for g in range(8)] for r in range(N)]
    x, c, L, s = [np.stack([np.stack([a[i] for a in row]) for row in t]) for i in range(4)]
    return {"cov": np.ascontiguousarray(x.reshape(N, 128, V)).astype(np.float32).astype(BF), "cand": np.stack([gtable(a.reshape(8, -1)) for a in L]),
            "shown": np.stack([gtable(a) for a in s]), "cur0": np.stack([gtable(a) for a in c])}
def plain(rng, r, g):
    c = rng.integers(0, K, E); L, free = blank()
    weave(rng, L, free, c, rng.permutation(V), rng.choice(np.array([0.01, 0.05, 0.15, 0.3, 0.5]))); fill(rng, L, free, closed([], 0))
    return cover(rng), c, L, show(rng, np.arange(E), [])
def uneven(rng, r, g):
    c = np.minimum((K * rng.random(E) ** rng.choice(np.array([0.25, 1.0, 4.0]))).astype(np.int64), K - 1); L, free = blank()
    weave(rng, L, free, c, rng.permutation(V), rng.choice(np.array([0.02, 0.1, 0.4, 0.8]))); fill(rng, L, free, closed([], 0))
    x = np.exp2(np.log2(CM + 1.0) * rng.random((1, V))) * rng.random((16, V)) ** rng.choice(np.array([0.25, 1.0, 3.0]), (16, 1))
    return np.minimum(x.astype(np.int64), CM), c, L, show(rng, np.arange(E), [])
def atends(rng, r, g):
    n = 2 ** J; m = G // 4; c = (K - 1) * rng.integers(0, 2, E); L, free = blank()
    lx, ly, lz = [n + (int(rng.choice(np.array([0, 0, 1, -1, -3]))) if g < 6 else 0) for i in range(3)]
    a, z = (V - 1, 0) if (r + g) % 2 == 0 else (0, V - 1)
    mid = rng.permutation(np.arange(m, V - m)); k = lx - 1 + ly
    X = np.append(mid[:lx - 1], a); Y = mid[lx - 1:k]; Z = np.append(mid[k:k + lz - 1], z); mid = mid[k + lz - 1:]
    f, e = duel(rng, L, free, c, X, Y, Z, (r + g) % RO, (r + 2 * g) % RO)
    weave(rng, L, free, c, rng.permutation(np.concatenate([mid, np.arange(1, m), np.arange(V - m, V - 1)])), rng.choice(np.array([0.05, 0.2, 0.4])))
    fill(rng, L, free, closed(np.concatenate([X, Y, Z]), 3))
    x = CM * (rng.random((16, V)) < rng.choice(np.array([0.0, 0.1, 0.5, 1.0]), (1, V))).astype(np.int64)
    paint(rng, x, X, Y, Z, NV[(5 * (N - 1 - r) + 7 - g) % 8], g % 2 == 0, False)
    last = [e ^ 1, f ^ 1, f]
    return x, c, L, show(rng, np.setdiff1d(np.concatenate([np.arange(2 * m), np.arange(E - 2 * m, E)]), last), last)
def corner(rng, r, g, role):
    n = 2 ** J; c = np.full(E, (0, 1, 2, 3, K - 1, K - 2)[(r + role) % 6] % K); L, free = blank(); o = rng.permutation(V)
    x = cover(rng); x[:, 0::5] = 0; x[:, 1::5] = CM; pool = np.arange(E); last = []; shut = closed([], 0)
    if role < 2: weave(rng, L, free, c, o, float((r + role) % 2))
    elif role == 2:
        h = V // 2; k = h + h // 2; pair(L, free, c, 0, 2 * o[:h], 2 * o[:h] + 1)
        u = np.concatenate([2 * o[h:k], 2 * o[h:k] + 1])
        for e in u: put(L, free, c[e], e, e)
        u = rng.permutation(u); w = len(u) // 4; pair(L, free, c, 1, u[:w], u[w:2 * w]); weave(rng, L, free, c, o[k:], 0.3)
    elif role == 3:
        k = 0; i = r
        while k < V:
            w = min((1, 2, n - 1, n, n + 1, 3, 2 * n)[i % 7], V - k); a, b = sides(rng, o[k:k + w]); pair(L, free, c, 0, a[:-1], b[1:])
            if rng.random() < 0.4: pair(L, free, c, 0, a[-1:], b[:1])
            k += w; i += 1
        u = rng.permutation(np.flatnonzero(L[c, np.arange(E)] < 0)); w = 3 * len(u) // 10; pair(L, free, c, 1, u[:w], u[w:2 * w])
    else:
        lx, ly, lz = [int(v) for v in rng.choice(np.array([1, 2, n - 1, n, n + 1]), 3)]; k = lx + ly + lz
        X, Y, Z = o[:lx], o[lx:lx + ly], o[lx + ly:k]
        f, e = duel(rng, L, free, c, X, Y, Z, (r + role) % RO, (r + g) % RO); weave(rng, L, free, c, o[k:], 0.3)
        paint(rng, x, X, Y, Z, NV[(3 * r + role) % 8], r % 2 == 1 and role < 6, role % 2 == 1)
        last = [f]; pool = np.concatenate([2 * o[k:], 2 * o[k:] + 1]); shut = closed(o[:k], 1)
    fill(rng, L, free, shut)
    return x, c, L, show(rng, pool, last)
def ballots(rng):
    a, b = K - 1, 2 * (K - 1); v = np.full((N, 8, 4, NI), 8); s = b + K * np.arange(2 * (N - 1))
    first = np.unique(np.concatenate([np.array([0, a - 1, a, b - 1]), s, s + K - 1]))
    one = np.concatenate([rng.permutation(first), rng.permutation(np.setdiff1d(np.arange(NI), first))]); u = rng.permutation(8 * N).reshape(N, 8)
    top = 16
    while 2 * top <= NI: top = 2 * top
    for q in range(N):
        for g in range(8):
            for h in range(4):
                kind = (g + h) % 4; o = rng.permutation(NI)
                if kind == 0: v[q, g, h, o[q % 2:]] = 16
                elif kind == 1: v[q, g, h, one[u[q, g] % NI]] = 9
                elif kind == 3:
                    w = (16, top)[q % 2]; v[q, g, h, o[:w]] = 15 + rng.integers(0, 2, w)
    return v
def crowd(rng, r, g, votes):
    n = 2 ** J; c = rng.integers(0, K, E); L, free = blank(); x = cover(rng); o = rng.permutation(V); k = 0; hubs = []
    for h in range(4):
        lx, ly = [int(v) for v in rng.integers(1, 6, 2)]; xy = o[k:k + lx + ly]; k += lx + ly
        a, b = join(rng, L, free, c, xy, lx); hubs.append((int(a[lx - 1]), int(b[lx]))); x[:, xy[:lx]] = CM; x[:, xy[lx:]] = 0
    lx, ly, lz = ((n - 1, n, n - 3), (n - 1, n - 3, n), (n - 3, n, n - 1), (n - 3, n - 1, n))[(r + g // 2) % 4]; w = o[k:k + lx + ly + lz]; k += len(w)
    fine(rng, L, free, c, x, w[:lx], w[lx:lx + ly], w[lx + ly:], (r + 2 * g) % RO, (9, 8)[(r + g) % 2], rng.random() < 0.5)
    shut = closed(o[:k], 8)
    for h, (f, b) in enumerate(hubs):
        t = h % RO; on = rng.permutation(16); mine = votes[r, g, h]
        jobs = [(i, f, CM, mine[j]) for j, i in enumerate([y for y in range(K) if y != c[b]])]
        jobs += [(i, b, 0, mine[K - 1 + j]) for j, i in enumerate([y for y in range(K) if y != c[f]])]
        jobs += [(i, E + d * G + G - 1 - h - 4 * s, CM * (1 - s), votes[(r - d - 1) % N, (g + 2) % 8, h, 2 * (K - 1) + (s * (N - 1) + d) * K + i]) for s in range(2) for d in range(N - 1) for i in range(K)]
        for j, (i, p, v, nv) in enumerate(jobs):
            z = int(o[k]); k += 1; e = 2 * z + (j + h) % 2; c[e] = (i - t) % K; put(L, free, i, e, p)
            x[:, z] = CM - v; x[on[:nv], z] = v
    weave(rng, L, free, c, o[k:], rng.choice(np.array([0.05, 0.2, 0.4]))); fill(rng, L, free, shut)
    return x, c, L, show(rng, np.concatenate([2 * o[k:], 2 * o[k:] + 1]), [b for f, b in hubs[::-1]] + [f for f, b in hubs[::-1]])
def setup_inputs(rng):
    return draw(rng, plain)
def setup_inputs_spread(rng):
    return draw(rng, uneven)
def setup_inputs_ends(rng):
    return draw(rng, atends)
def setup_inputs_corners(rng):
    role = np.zeros(8, np.int64); p = int(rng.integers(0, 2)); role[p::2] = 4 + rng.permutation(4); role[1 - p::2] = rng.permutation(4)
    return draw(rng, lambda rng, r, g: corner(rng, r, g, int(role[g])))
def setup_inputs_crowd(rng):
    votes = ballots(rng)
    return draw(rng, lambda rng, r, g: crowd(rng, r, g, votes))
def check_inputs(d):
    bad = []
    x = np.asarray(d["cov"]).astype(np.float64)
    if not (np.all(x >= 0) and np.all(x <= CM) and np.all(x == np.floor(x))): bad.append("range of cov")
    for k, hi in (("cand", P - 1), ("shown", E - 1), ("cur0", K - 1)):
        if np.min(d[k]) < 0 or np.max(d[k]) > hi: bad.append("range of " + k)
    for k, m in (("cand", E), ("shown", G)):
        a = np.sort(np.stack([gentries(t) for t in d[k]]).reshape(N, 8, -1, m), axis=-1)
        if np.any(a[..., 1:] == a[..., :-1]): bad.append("a number twice in " + k)
    return bad
def seen(a, sl):
    s = np.take_along_axis(a, sl if a.ndim == 3 else sl[:, :, None, :], -1)
    return np.stack([np.concatenate([a[r]] + [np.roll(s[(r - d) % N], -2, axis=0) for d in range(1, N)], axis=-1) for r in range(N)])
def reference(cov, cand, shown, cur0):
    pick = np.take_along_axis; ar = np.arange(E)
    x = np.repeat(cov.astype(np.float32).astype(np.int32).reshape(N, 8, 16, V), 2, axis=3)
    x = np.concatenate([x, np.zeros((N, 8, 16, 1), np.int32)], axis=3)
    cl = np.stack([gentries(a) for a in cand]).astype(np.int64).reshape(N, 8, K, E)
    sl = np.stack([gentries(a) for a in shown]).astype(np.int64); c = np.stack([gentries(a) for a in cur0]).astype(np.int64)
    for rnd in range(RO):
        b = pick(cl, c[:, :, None, :], 2)[:, :, 0]
        own = b < E
        link = own & (b != ar) & (pick(b, np.where(own, b, ar), 2) == ar)
        nx = np.concatenate([np.where(link, b ^ 1, E), np.full((N, 8, 1), E)], axis=2)
        S = x; n = np.concatenate([np.ones((N, 8, E), np.int32), np.zeros((N, 8, 1), np.int32)], axis=2)
        for j in range(J):
            S = S + pick(S, nx[:, :, None, :], 3); n = n + pick(n, nx, 2); nx = pick(nx, nx, 2)
        w = S[..., ar ^ 1]; m = n[..., ar ^ 1]; pt = np.where(link, b, ar)
        wp = pick(w, pt[:, :, None, :], 3); mp = pick(m, pt, 2)
        bw = b[:, :, None, :]
        wf = pick(seen(w, sl), bw, 3); wh = pick(seen(wp, sl), bw, 3)
        mf = pick(seen(m, sl), b, 2)[:, :, None, :]; mh = pick(seen(mp, sl), b, 2)[:, :, None, :]; lf = pick(seen(link, sl), b, 2)
        m1 = m[:, :, None, :]
        vote = np.abs(w * mf - wf * m1) * mh < np.abs(wh * mf - wf * mh) * m1
        cut = ~link & lf & (np.add.reduce(vote.astype(np.int32), axis=2) >= NEED)
        hit = np.zeros((N, 8, P), bool)
        for r in range(N):
            for g in range(8): hit[r, g, b[r, g][cut[r, g]]] = True
        gone = np.array(hit[:, :, :E])
        for q in range(N):
            for d in range(1, N):
                for g in range(8): gone[q, g, sl[q, g][hit[(q + d) % N, (g - 2) % 8, E + (d - 1) * G:E + d * G]]] = True
        gone = gone | pick(gone, pt, 2)
        c = (c + (~link | gone).astype(np.int64)) % K
    return {"yc": np.stack([gtable(a) for a in c]).astype(np.float32), "ys": np.ascontiguousarray(S[..., :E]).reshape(N, 128, E).astype(np.float32)}

@@ -1,0 +1,595 @@
+import math
+from concourse.bass import DstId, RemoteDMATransfer
+from concourse.mybir import AluOpType as ALU, ActivationFunctionType as AF
+
+N, RO = 4, 4
+E, H, GH = 2048, 1024, 256
+O = 16
+OG = O + E
+W = OG + (N - 1) * GH
+LW = W // 16 + 1
+F32, BF, I32, U16, F16 = "float32", "bfloat16", "int32", "uint16", "float16"
+
+SCRATCH = {}
+def _b(dtype, cols, *names):
+    for n in names:
+        SCRATCH[n] = ("sbuf", [128, cols], dtype)
+_b(I32, 512, "candI", "hI")
+_b(I32, 128, "curI", "tI", "bitI", "lI", "selfI", "bn0", "bn1")
+_b(I32, 16, "shI", "shH")
+_b(I32, 8, "colI")
+_b(F32, 8, "colF", "colP")
+_b(F32, 16, "shA", "shB")
+_b(F16, 512, "c1h", "h1h", "uh", "FA", "FB", "FC")
+_b(BF, 128, "curB", "IDB", "ID4", "SHP", "xc", "cB")
+_b(BF, 512, "FF", "FI")
+_b(F32, 128, "SHM", "cF", "bF", "pt", "unl", "u0", "nm", "stayb", "tmp", "tmp2", "dc", "xe", "ycs", "P2", "P2q", "P2m", "dP")
+_b(BF, 128, "P2n0", "P2n1")
+_b(BF, 144, "Z1", "ZP", "ZD", "Z0")
+_b(BF, H, "covB")
+_b(F32, 512, "CAND", "MK", "SG")
+_b(F32, OG, "C", "YA", "YB")
+_b(F32, W, "YF", "DW")
+_b(BF, W, "MW", "HW", "TT")
+_b(BF, OG, "N0", "NA", "NB", "TD", "RW")
+_b(BF, 688, "TL")
+_b(BF, 708, "ZB")
+_b(F32, E, "IO", "GA", "YS")
+_b(BF, E, "EQ", "EQ2", "V", "CUT")
+_b(BF, 144, "ONE")
+_b(F32, 128, "tmp3")
+_b(BF, 4 * W, "SW")
+_b(F32, LW + 7, "LWN")
+_b(BF, LW + 7, "GW", "MV")
+_b(U16, 128, "ptu", "LA", "LB", "bu", "bmu", "slu", "hiu", "hin")
+_b(U16, 48, "shu")
+_b(BF, GH, "PS", "R1")
+_b(BF, 2 * GH, "tf")
+_b(F32, GH, "sa", "sb")
+_b(BF, 3 * GH, "HR")
+for _r in range(RO):
+    _b(F32, GH, "SY%d" % _r, "SD%d" % _r)
+    _b(BF, 2 * GH, "SM%d" % _r)
+    _b(BF, 3 * GH, "SH%d" % _r)
+for _k in range(4):
+    SCRATCH["PA%d" % _k] = ("psum", [128, 512], F32)
+    SCRATCH["PB%d" % _k] = ("psum", [128, 512], F32)
+
+SEMAPHORES = ["sv", "sa", "sp", "sg", "sent", "ldc", "ldu", "lds", "ldv", "ldt", "ldz", "sty", "stc"] + \
+    ["%s%d" % (k, r) for k in ("ay", "ad", "am", "ah") for r in range(RO)]
+ENG_SEM = {"v": "sv", "a": "sa", "p": "sp", "g": "sg"}
+CG = 768
+
+
+def rank_program(g, core, T, topo):
+    rank = T.rank_of(core)
+    if rank is None:
+        return
+    Q = {"v": g.vector, "a": g.scalar, "p": g.tensor, "g": g, "s": g.sync}
+    ops = []
+
+    def vw(name, lo=0, hi=None, step=1):
+        return (name, lo, SCRATCH[name][1][1] if hi is None else hi, step)
+
+    def ap(v):
+        if len(v) == 2:
+            return ap(v[0]).indirect(ap(v[1]))
+        return T[v[0]][:, v[1]:v[2]] if v[3] == 1 else T[v[0]][:, v[1]:v[2]:v[3]]
+
+    def parts(v):
+        return [v[0], v[1]] if len(v) == 2 else [v]
+
+    def isv(x):
+        return isinstance(x, tuple)
+
+    def val(x):
+        return ap(x) if isv(x) else x
+
+    def rec(q, fn, out, ins, waits=(), dma=None):
+        rd, wr = [], []
+        for v in ins:
+            if isv(v):
+                rd += parts(v)
+        for v in out:
+            if len(v) == 2:
+                wr.append(v[0]); rd.append(v[1])
+            else:
+                wr.append(v)
+        ops.append({"q": q, "fn": fn, "rd": rd, "wr": wr, "waits": list(waits), "dma": dma})
+
+    def tt(out, a, b, op, waits=()):
+        rec("v", lambda: g.vector.tensor_tensor(ap(out), ap(a), ap(b), op), [out], [a, b], waits)
+
+    def ts(out, a, s1, op0, s2=None, op1=None, waits=()):
+        if op1 is None:
+            rec("v", lambda: g.vector.tensor_scalar(ap(out), ap(a), val(s1), None, op0), [out], [a, s1], waits)
+        else:
+            rec("v", lambda: g.vector.tensor_scalar(ap(out), ap(a), val(s1), val(s2), op0, op1), [out], [a, s1, s2], waits)
+
+    def cp(out, a, waits=()):
+        rec("v", lambda: g.vector.tensor_copy(ap(out), ap(a)), [out], [a], waits)
+
+    def ms(out, c):
+        rec("v", lambda: g.vector.memset(ap(out), c), [out], [])
+
+    def act(out, a, f=AF.Copy, bias=None, scale=None, waits=()):
+        kw = {}
+        if bias is not None:
+            kw["bias"] = bias
+        if scale is not None:
+            kw["scale"] = scale
+        rec("a", lambda: g.scalar.activation(ap(out), ap(a), f, **kw), [out], [a], waits)
+
+    def mm(out, l, r, st, sp):
+        rec("p", lambda: g.tensor.matmul(ap(out), ap(l), ap(r), st, sp), [out], [l, r])
+
+    def asel(out, a, pat, op, base, cm):
+        rec("g", lambda: g.affine_select(ap(out), ap(a), pat, op, 0.0, base, cm), [out], [a])
+
+    def iota(out, pat, base, cm, flt):
+        if flt:
+            rec("g", lambda: g.iota(ap(out), pat, base, cm, allow_small_or_imprecise_dtypes=True), [out], [])
+        else:
+            rec("g", lambda: g.iota(ap(out), pat, base, cm), [out], [])
+
+    def dma(q, o, i, sem, out, ins):
+        rec(q, lambda: Q[q].dma_start(o(), i()), out, ins, dma=sem)
+
+    def conv(out, z, name, lo, n, first=True, last=True):
+        for i in range(16):
+            mm(out, vw(z, 16 - i, 144 - i), vw(name, lo + i, lo + i + 16 * (n - 1) + 1, 16), first and i == 0, last and i == 15)
+
+    def peer(d):
+        return T.cores[(rank + d) % N]
+    free = {}
+    order = sorted(range(1, N), key=lambda d: len(topo.engines(core, peer(d))))
+    narrow = [d for d in order if len(topo.engines(core, peer(d))) == len(topo.engines(core, peer(order[0])))]
+    used = []
+    for d in order:
+        left = [e for e in topo.engines(core, peer(d)) if e not in used]
+        k = len(topo.engines(core, peer(d))) // len(narrow) if d in narrow else len(left)
+        k = 1 << (k.bit_length() - 1)
+        free[d] = left[:k]
+        used += left[:k]
+    nsent = [0]
+
+    def arrivals():
+        return sum(len(v) for v in free.values())
+
+    def send(items, sem):
+        def fn():
+            tr = []
+            share = len(items) // (N - 1)
+            for j, (d, s, t) in enumerate(items):
+                rid, pid = topo.addr(peer(d), core)
+                mine = free[d][j // (N - 1)::share]
+                tr.append(RemoteDMATransfer(dst_ids=[DstId(rid=rid, pnc=pid)], dma_engine_mask=sum(1 << e for e in mine),
+                                            remote_sem=T.sem[sem], src=ap(s), dst=ap(t)))
+            return g.remote_dma_fused(tr, local_sem=T.sem["sent"])
+        rec("g", fn, [], [s for d, s, t in items], dma="remote")
+        nsent[0] += arrivals()
+
+    PA = ["PA%d" % k for k in range(4)]
+    PB = ["PB%d" % k for k in range(4)]
+    BIG = 1000
+    LN2 = math.log(2.0)
+    UNP = 128.4921875
+
+    dma("s", lambda: T.candI[:, :], lambda: T.cand[:, :], "ldc", [vw("candI")], [])
+    dma("a", lambda: T.curI[:, :], lambda: T.cur0[:, :], "ldu", [vw("curI")], [])
+    dma("a", lambda: T.covB[:, :], lambda: T.cov[:, :], "ldv", [vw("covB")], [])
+    dma("s", lambda: T.shI[:, :], lambda: T.shown[:, :], "lds", [vw("shI")], [])
+    ms(vw("ONE", 0, 144), 1.0)
+    for s in range(2):
+        for par in range(2):
+            k = 2 * s + par
+            asel(vw("FF", 128 * k, 128 * k + 128), vw("ONE", 0, 128), [[-16, 8], [BIG, 2], [-2, 8]], ALU.is_equal, -s - BIG * par, 1)
+    iota(vw("colI", 0, 1), [[0, 1]], 0, 1, False)
+    iota(vw("selfI"), [[16, 128]], O, 0, False)
+    asel(vw("Z0"), vw("ONE", 0, 144), [[-16, 9], [-BIG, 16]], ALU.is_ge, 16, 1)
+    asel(vw("Z1"), vw("Z0"), [[16, 9], [0, 16]], ALU.is_ge, -1, -1)
+    iota(vw("IO"), [[1, E]], O, 0, True)
+    iota(vw("TD"), [[16, OG // 16], [0, 16]], 0, 0, True)
+    iota(vw("TL"), [[0, 43], [1, 16]], 0, 0, True)
+    for k in range(3):
+        dma("s", lambda k=k: T.TD[1:128:16, 688 * k:688 * k + 688], lambda: T.TL[1:128:16, :], "ldt",
+            [vw("TD", 688 * k, 688 * k + 688)], [vw("TL")])
+    asel(vw("ZD"), vw("Z0"), [[16, 9], [0, 16]], ALU.is_ge, -15, -1)
+    ms(vw("ZB"), 0.0)
+    ms(vw("C", 0, O), -4096.0)
+    for name in ("YA", "YB", "YF", "DW", "MW", "HW", "N0", "NA", "NB"):
+        ms(vw(name, 0, O), 0.0)
+    for name in ("LWN", "GW", "MV"):
+        ms(vw(name), 0.0)
+    cp(vw("FC"), vw("FF"))
+    ts(vw("colI", 1, 2), vw("colI", 0, 1), 15, ALU.bitwise_and)
+    ts(vw("uh"), vw("candI"), -1024.0, ALU.add)
+    cp(vw("colF", 0, 1), vw("colI", 1, 2))
+    ts(vw("FA"), vw("FF"), 1023.0, ALU.mult)
+    act(vw("ID4", 0, 1), vw("colF", 0, 1), AF.Exp, scale=LN2)
+    ts(vw("c1h"), vw("candI"), 2047.0, ALU.min)
+    ts(vw("hI"), vw("candI"), 1, ALU.arith_shift_right)
+    ts(vw("FB"), vw("FF"), -2047.0, ALU.mult)
+    ts(vw("h1h"), vw("hI"), 1023.0, ALU.min)
+    cp(vw("curB"), vw("curI"))
+    for n, (f, x) in enumerate((("FC", "uh"), ("FA", "c1h"), ("FB", "h1h"))):
+        for s in range(2):
+            for par in range(2):
+                k = 2 * s + par
+                mm(vw(PA[s], 0, 256), vw(f, 128 * k, 128 * k + 128), vw(x, par, 511 + par, 2), n + par == 0, n + par == 3)
+    for s in range(2):
+        for par in range(2):
+            k = 2 * s + par
+            mm(vw(PA[2], 64 * s, 64 * s + 64), vw("FF", 128 * k, 128 * k + 128), vw("curB", par, 127 + par, 2), par == 0, par == 1)
+    for s in range(2):
+        for i in range(4):
+            act(vw("CAND", 128 * i + 64 * s, 128 * i + 64 * s + 64), vw(PA[s], 64 * i, 64 * i + 64), AF.Identity, bias=float(1024 + O))
+    ts(vw("selfI"), vw("selfI"), vw("colF", 0, 1), ALU.add)
+    cp(vw("cF"), vw(PA[2], 0, 128))
+    cp(vw("colP", 0, 1), vw("ID4", 0, 1))
+
+    def nxt_a(shift):
+        for i in range(4):
+            ts(vw("MK", 128 * i, 128 * i + 128), vw("cF"), float((i - shift) % 4), ALU.is_equal)
+        if shift:
+            ts(vw("dc"), vw("MK", 0, 128), -4.0, ALU.mult, 1.0, ALU.add)
+
+    def nxt_b():
+        tt(vw("MK"), vw("MK"), vw("CAND"), ALU.mult)
+
+    def nxt_c(k):
+        tt(vw("MK", 0, 256), vw("MK", 0, 256), vw("MK", 256, 512), ALU.add)
+        tt(vw("bn%d" % k), vw("MK", 0, 128), vw("MK", 128, 256), ALU.add)
+
+    def nxt_d(k):
+        bn = vw("bn%d" % k)
+        tt(vw("tmp3"), bn, vw("selfI"), ALU.not_equal)
+        ts(vw("lI"), bn, 15, ALU.bitwise_and)
+        ts(vw("hin"), bn, 1.0 / 16, ALU.mult, -0.46875, ALU.add)
+        tt(vw("LWN", 1, 129), bn, vw("tmp3"), ALU.mult)
+        ts(vw("xe"), vw("lI"), -LN2, ALU.mult, 15 * LN2, ALU.add)
+        act(vw("P2n%d" % k), vw("xe"), AF.Exp)
+
+    def mutual_gather(*hs):
+        for h in hs:
+            tt(vw("EQ2", H * h, H * h + H), (vw("LWN"), vw("hin", 64 * h, 64 * h + 64)), vw("IO", H * h, H * h + H), ALU.is_equal)
+
+    def mutual_conv(bank):
+        for h in range(2):
+            conv(vw(bank, 64 * h, 64 * h + 64), "ZP", "EQ2", H * h, 64)
+
+    def bit(bank, p2):
+        tt(vw("tI"), vw(bank, 0, 128), p2, ALU.mult)
+        ts(vw("bitI"), vw("tI"), 15, ALU.arith_shift_right, 1, ALU.bitwise_and)
+
+    def look(win, offs, bank):
+        for h in range(2):
+            cp(vw("EQ", H * h, H * h + 512), (vw(win), vw(offs, 64 * h, 64 * h + 32)))
+            act(vw("EQ", H * h + 512, H * h + H), (vw(win), vw(offs, 64 * h + 32, 64 * h + 64)))
+            conv(vw(bank, 64 * h, 64 * h + 64), "ZP", "EQ", H * h, 64)
+
+    nxt_a(0)
+    ts(vw("ZP"), vw("Z1"), vw("colP", 0, 1), ALU.mult)
+    nxt_b()
+    nxt_c(1)
+    nxt_d(1)
+    mutual_gather(0, 1)
+    mutual_conv(PA[3])
+    for h in range(2):
+        act(vw("C", O + H * h, O + H * h + H), vw("covB"), AF.Identity, bias=-8192.0)
+    ts(vw("shH"), vw("shI"), 1, ALU.arith_shift_right)
+    ts(vw("shB"), vw("shI"), 1024.0, ALU.mult)
+    ts(vw("shA"), vw("shH"), -2047.0, ALU.mult, float(O), ALU.add)
+    tt(vw("shA"), vw("shA"), vw("shB"), ALU.add)
+    bit(PA[3], vw("P2n1"))
+    tt(vw("pt"), vw("bitI"), vw("bn1"), ALU.mult)
+    cp(vw("ptu"), vw("pt"))
+    for k in range(16):
+        dma("s", lambda k=k: T.SW[:, 708 * k:708 * k + 708], lambda: T.ZB[:, :], "ldz", [vw("SW", 708 * k, 708 * k + 708)], [vw("ZB")])
+    for k in range(3):
+        dma("s", lambda k=k: T.RW[:, 688 * k:688 * k + 688], lambda: T.ZB[:, 0:688], "ldz", [vw("RW", 688 * k, 688 * k + 688)], [vw("ZB")])
+    asel(vw("SHM", 0, 96), vw("ONE", 0, 96), [[-1, 96]], ALU.is_equal, -32, 1)
+    asel(vw("SHM", 96, 128), vw("ONE", 0, 32), [[-1, 32]], ALU.is_equal, 0, 1)
+    asel(vw("IDB"), vw("ONE", 0, 128), [[-1, 128]], ALU.is_equal, 0, 1)
+    asel(vw("SHP", 0, 32), vw("ONE", 0, 32), [[-16, 2], [BIG, 16]], ALU.is_equal, -96, 1)
+    asel(vw("SHP", 32, 128), vw("ONE", 0, 96), [[-16, 6], [BIG, 16]], ALU.is_equal, 0, 1)
+    for s in range(2):
+        for par in range(2):
+            k = 2 * s + par
+            asel(vw("FI", 128 * k, 128 * k + 128), vw("ONE", 0, 128), [[-16, 8], [-1, 8], [BIG, 2]], ALU.is_equal, -8 * par - BIG * s, 1)
+
+    for r in range(RO):
+        st = float(64 ** r)
+        last = r == RO - 1
+        kc, kn = (r + 1) % 2, r % 2
+        half = lambda name, h: vw(name, O + H * h, O + H * h + H)
+        lists = lambda name, h: vw(name, 64 * h, 64 * h + 64)
+        first = lambda h: vw("ptu", 64 * (1 - h), 64 * (1 - h) + 64)
+        cp(half("N0", 0), (vw("TD"), first(0)))
+        act(half("N0", 1), (vw("TD"), first(1)))
+        if r == 0:
+            ts(vw("shB"), vw("shA"), float(O + H), ALU.is_ge, -2.0 * H, ALU.mult)
+            cp(vw("shu", 0, 16), vw("shA"))
+            tt(vw("shB"), vw("shB"), vw("shA"), ALU.add)
+            ts(vw("shu", 32, 48), vw("shB"), float(H), ALU.add)
+        ys_ = ["C", "YA", "YB", "YA", "YB", "YA", "YF"]
+        yc_ = [None, "GA", "YS", "GA", "YS", "GA"]
+        ns_ = ["N0", "NA", "NB", "NA", "NB", "NA"]
+        ls_ = [None, "LA", "LB", "LA", "LB", "LA"]
+        ch = lambda name, q, o=O: vw(name, o + 512 * q, o + 512 * q + 512)
+        lb = lambda name, q: vw(name, 32 * q, 32 * q + 32)
+
+        def add(k, q):
+            own = ch("covB", q % 2, 0) if k == 1 else ch(yc_[k - 1], q, 0)
+            tt(ch(ys_[k], q), (vw(ys_[k - 1], 0, OG), lb("ptu", q ^ 2) if k == 1 else lb(ls_[k - 1], q)), own, ALU.add)
+
+        def hop(k, h):
+            act(half(ns_[k], h), (vw(ns_[k - 1]), first(h) if k == 1 else lists(ls_[k - 1], h)))
+            conv(vw(PB[2 * (k % 2) + h], 0, 64), "ZD", ns_[k], O + H * h, 64)
+
+        def take(k, h):
+            cp(lists(ls_[k], h), vw(PB[2 * (k % 2) + h], 0, 64))
+
+        def twin_g(k, h):
+            asel(vw(yc_[k], H * h, H * h + CG), vw(ys_[k], O + H * h, O + H * h + CG), [[0, CG]], ALU.is_ge, 0, 0)
+
+        def twin_a(k, h):
+            act(vw(yc_[k], H * h + CG, H * h + H), vw(ys_[k], O + H * h + CG, O + H * h + H))
+
+        for k in range(1, 7):
+            if k < 6:
+                hop(k, 0)
+            else:
+                act(vw("PS"), (vw("N0"), vw("shu", 32, 48)))
+                conv(vw(PA[0], 0, 16), "ZD", "PS", 0, 16)
+            if k > 1:
+                twin_a(k - 1, 1)
+            add(k, 0)
+            if k > 1:
+                take(k - 1, 1)
+            add(k, 1)
+            if k < 6:
+                twin_g(k, 0)
+                hop(k, 1)
+                twin_a(k, 0)
+            else:
+                act(half("TT", 0), half("YF", 0), AF.Identity, bias=UNP, scale=-1.0 / 4096)
+                act(half("MW", 0), half("TT", 0), AF.Identity, bias=-128.0)
+            add(k, 2)
+            if k < 6:
+                take(k, 0)
+            else:
+                cp(vw("shu", 16, 32), vw(PA[0], 0, 16))
+            add(k, 3)
+            if k < 6:
+                twin_g(k, 1)
+        SY, SD, SM, SH = "SY%d" % r, "SD%d" % r, "SM%d" % r, "SH%d" % r
+        cp(vw("SG", 0, GH), (vw("YF", 0, OG), vw("shu", 0, 16)))
+        mm(vw(PA[0], 0, GH), vw("SHM"), vw("SG", 0, GH), True, True)
+        cp(vw("SG", GH, 2 * GH), (vw("YF", 0, OG), vw("shu", 16, 32)))
+        mm(vw(PA[1], 0, GH), vw("SHM"), vw("SG", GH, 2 * GH), True, True)
+        cp(vw(SY), vw(PA[0], 0, GH))
+        gz = lambda name, d: vw(name, OG + GH * (d - 1), OG + GH * d)
+        send([(d, vw(SY), gz("YF", d)) for d in range(1, N)], "ay%d" % r)
+        act(half("TT", 1), half("YF", 1), AF.Identity, bias=UNP, scale=-1.0 / 4096)
+        act(vw("tf", 0, GH), vw(SY), AF.Identity, bias=UNP, scale=-1.0 / 4096)
+        act(vw("tf", GH, 2 * GH), vw(PA[1], 0, GH), AF.Identity, bias=UNP, scale=-1.0 / 4096)
+        act(vw(SM), vw("tf"), AF.Identity, bias=-128.0)
+        send([(d, vw(SM, 0, GH), gz("MW", d)) for d in range(1, N)] + [(d, vw(SM, GH, 2 * GH), gz("HW", d)) for d in range(1, N)],
+             "am%d" % r)
+        act(half("MW", 1), half("TT", 1), AF.Identity, bias=-128.0)
+        for q in range(4):
+            act(vw(PB[q]), ch("YF", q))
+        if r == 0:
+            cp(vw("bF"), vw("bn1"))
+        else:
+            tt(vw("tmp"), vw("MV", 1, 129), vw("bn%d" % kc), ALU.mult)
+            tt(vw("tmp2"), vw("MV", 1, 129), vw("dc"), ALU.mult)
+            tt(vw("bF"), vw("tmp"), vw("stayb"), ALU.add)
+            tt(vw("cF"), vw("cF"), vw("tmp2"), ALU.add)
+        cp(vw("bu"), vw("bF"))
+        tt(vw("sa"), vw(SM, 0, GH), vw(PA[1], 0, GH), ALU.mult)
+        tt(vw("sb"), vw(SY), vw(SM, GH, 2 * GH), ALU.mult)
+        for q in (2, 3, 0, 1):
+            mm(vw(PA[q]), vw("IDB"), ch("MW", q), True, True)
+        tt(vw("tmp"), vw("bF"), vw("pt"), ALU.subtract)
+        tt(vw(SD), vw("sa"), vw("sb"), ALU.subtract)
+        send([(d, vw(SD), gz("DW", d)) for d in range(1, N)], "ad%d" % r)
+        ts(vw("tmp2"), vw("cF"), float(W), ALU.mult)
+        cp(vw("bmu"), vw("tmp"))
+        tt(vw("tmp2"), vw("tmp2"), vw("bF"), ALU.add)
+        if not last:
+            nxt_a(1)
+        cp(vw("slu"), vw("tmp2"))
+        if r:
+            tt(vw("dP"), vw("P2n%d" % kc), vw("P2"), ALU.subtract)
+        wy, wd, wm = [[("%s%d" % (x, r), arrivals())] for x in ("ay", "ad", "am")]
+        def f_a(q):
+            act(ch("GA", q, 0), (vw("YF"), lb("bu", q)), waits=wy)
+            tt(ch("YA", q), ch("GA", q, 0), vw(PA[q]), ALU.mult)
+
+        def f_b(q):
+            act(ch("HW", q), (vw("MW"), lb("bu", q)), waits=wm)
+            tt(vw(PB[q]), ch("HW", q), vw(PB[q]), ALU.mult)
+            tt(ch("DW", q), ch("YA", q), vw(PB[q]), ALU.subtract)
+        if not last:
+            nxt_b()
+        f_a(0); f_a(1); f_b(0); f_b(1); f_a(2); f_b(2); f_a(3); f_b(3)
+
+        def s_0(q):
+            act(vw(PB[q]), ch("DW", q), AF.Abs)
+
+        def s_a(q):
+            act(ch("GA", q, 0), (vw("DW"), lb("bmu", q)), AF.Abs, waits=wd)
+            act(ch("EQ", q, 0), (vw("HW"), lb("bmu", q)))
+
+        def s_b(q):
+            tt(ch("YB", q), ch("GA", q, 0), vw(PA[q]), ALU.mult)
+            tt(vw(PB[q]), ch("EQ", q, 0), vw(PB[q]), ALU.mult)
+            tt(ch("V", q, 0), ch("YB", q), vw(PB[q]), ALU.is_gt)
+            mm(vw(PB[q]), vw("Z1", 16, 144), ch("V", q, 0), True, True)
+
+        def s_d(q):
+            act(ch("CUT", q, 0), vw(PB[q]), AF.Relu, bias=-8.0 * st, scale=st)
+
+        def s_e(q):
+            cp((vw("SW"), lb("slu", q)), ch("CUT", q, 0))
+        s_0(0); s_0(1)
+        if not last:
+            nxt_c(kn)
+        s_a(0); s_b(0); s_a(1); s_d(0); s_b(1); s_0(2); s_a(2); s_e(0); s_d(1); s_b(2); s_0(3); s_a(3)
+        s_e(1); s_d(2); s_b(3); s_d(3); s_e(2); s_e(3)
+        for d in range(1, N):
+            for i in range(4):
+                lo = i * W + OG + GH * (d - 1)
+                mm(vw(PA[d - 1], 0, GH), vw("SHP"), vw("SW", lo, lo + GH), i == 0, i == 3)
+            o = vw(SH, GH * (d - 1), GH * d)
+            if d == 2:
+                act(o, vw(PA[d - 1], 0, GH), AF.Relu, bias=(1.0 - st) * st, scale=st)
+            else:
+                ts(o, vw(PA[d - 1], 0, GH), st, ALU.is_ge, st, ALU.mult)
+        send([(N - d, vw(SH, GH * (d - 1), GH * d), vw("HR", GH * (d - 1), GH * d)) for d in range(1, N)], "ah%d" % r)
+        if last:
+            ts(vw("ID4"), vw("IDB"), 4096.0, ALU.mult)
+            for q in range(4):
+                mm(vw(PB[q]), vw("ID4"), ch("MW", q), True, True)
+                lo = 2 * 512 * (q % 2) + 1 - q // 2
+                tt(vw("YS", lo, lo + 1023, 2), ch("YF", q), vw(PB[q]), ALU.add)
+            dma("s", lambda: T.ys[:, :], lambda: T.YS[:, :], "sty", [], [vw("YS")])
+        for i in range(4):
+            conv(vw(PA[3], 0, 128), "Z1", "SW", i * W + O, 128, first=i == 0, last=False)
+        if not last:
+            nxt_d(kn)
+            mutual_gather(0, 1)
+            mutual_conv(PB[0])
+        else:
+            ts(vw("dc"), vw("cF"), 3.0, ALU.is_equal, -4.0, ALU.mult)
+            cp(vw("cB"), vw("cF"))
+            ts(vw("dc"), vw("dc"), 1.0, ALU.add)
+        tt(vw("R1"), vw("HR", 0, GH), vw("HR", GH, 2 * GH), ALU.add, waits=[("ah%d" % r, arrivals())])
+        tt((vw("RW"), vw("shu", 0, 16)), vw("R1"), vw("HR", 2 * GH, 3 * GH), ALU.add)
+        conv(vw(PA[3], 0, 128), "Z1", "RW", O, 128, first=False, last=True)
+        ts(vw("hiu"), vw("pt"), 1.0 / 16, ALU.mult, -0.46875, ALU.add)
+        if r == 0:
+            cp(vw("P2"), vw("P2n1"))
+        else:
+            tt(vw("tmp"), vw("MV", 1, 129), vw("dP"), ALU.mult)
+        ts(vw("unl"), vw("pt"), 0.0, ALU.is_equal)
+        if r:
+            tt(vw("P2"), vw("P2"), vw("tmp"), ALU.add)
+        ts(vw("GW", 1, 129), vw(PA[3], 0, 128), st, ALU.is_ge)
+        look("GW", "hiu", PA[0])
+        tt(vw("u0"), vw("GW", 1, 129), vw("unl"), ALU.max)
+        if not last:
+            tt(vw("lI"), vw(PB[0], 0, 128), vw("P2n%d" % kn), ALU.mult)
+        tt(vw("tI"), vw(PA[0], 0, 128), vw("P2"), ALU.mult)
+        if not last:
+            ts(vw("lI"), vw("lI"), 15, ALU.arith_shift_right, 1, ALU.bitwise_and)
+        ts(vw("bitI"), vw("tI"), 15, ALU.arith_shift_right, 1, ALU.bitwise_and)
+        if not last:
+            tt(vw("P2q"), vw("lI"), vw("P2n%d" % kn), ALU.mult)
+        tt(vw("MV", 1, 129), vw("bitI"), vw("u0"), ALU.max)
+        if not last:
+            look("MV", "hin", PA[1])
+            ts(vw("nm"), vw("MV", 1, 129), -1.0, ALU.mult, 1.0, ALU.add)
+            tt(vw("P2m"), vw("P2q"), vw("MV", 1, 129), ALU.mult)
+            tt(vw("stayb"), vw("nm"), vw("bF"), ALU.mult)
+            bit(PA[1], vw("P2m"))
+            tt(vw("tmp"), vw("bitI"), vw("bn%d" % kn), ALU.mult)
+            tt(vw("pt"), vw("tmp"), vw("stayb"), ALU.add)
+            cp(vw("ptu"), vw("pt"))
+        else:
+            tt(vw("xc"), vw("MV", 1, 129), vw("dc"), ALU.mult)
+            for par in range(2):
+                n = 0
+                for x in ("cB", "xc"):
+                    for s in range(2):
+                        k = 2 * s + par
+                        mm(vw(PB[par], 0, 64), vw("FI", 128 * k, 128 * k + 128), vw(x, 64 * s, 64 * s + 64), n == 0, n == 3)
+                        n += 1
+            cp(vw("ycs", 0, 127, 2), vw(PB[0], 0, 64))
+            act(vw("ycs", 1, 128, 2), vw(PB[1], 0, 64))
+            dma("s", lambda: T.yc[:, :], lambda: T.ycs[:, :], "stc", [], [vw("ycs")])
+
+    def meet(a, b):
+        return a[0] == b[0] and (a[0][0] == "P" and a[0][1] in "AB" and len(a[0]) == 3 or (a[1] < b[2] and b[1] < a[2]))
+
+    def psum(v):
+        return SCRATCH[v[0]][0] == "psum"
+
+    hist = {}
+    deps, clock, known = [], [], {}
+    for n, o in enumerate(ops):
+        dep = set()
+        isdma = o["dma"] is not None
+        for v, w in [(v, False) for v in o["rd"]] + [(v, True) for v in o["wr"]]:
+            for m, u, uw in hist.get(v[0], []):
+                p = ops[m]
+                if not meet(u, v):
+                    continue
+                same = p["q"] == o["q"] and p["dma"] is None and not isdma
+                exact = u[1] < v[2] and v[1] < u[2]
+                if same:
+                    if o["q"] != "p" and exact and (uw or w):
+                        dep.add(m)
+                elif w or uw or psum(v):
+                    if p["dma"] != "remote" and not (isdma and p["dma"] == o["dma"]):
+                        dep.add(m)
+        for v in o["wr"]:
+            if v[3] == 1:
+                hist[v[0]] = [x for x in hist.get(v[0], []) if not (v[1] <= x[1][1] and x[1][2] <= v[2] and not psum(v))]
+            hist.setdefault(v[0], []).append((n, v, True))
+        for v in o["rd"]:
+            hist.setdefault(v[0], []).append((n, v, False))
+        best = {}
+        for m in dep:
+            key = ops[m]["dma"] or ops[m]["q"]
+            best[key] = max(best.get(key, -1), m)
+        kn_ = known.setdefault(o["q"], {})
+        for key in sorted(best, key=lambda x: -best[x]):
+            m = best[key]
+            if kn_.get(key, -1) >= m:
+                del best[key]
+                continue
+            kn_[key] = m
+            for x, y in clock[m].items():
+                kn_[x] = max(kn_.get(x, -1), y)
+        clock.append(dict(kn_))
+        deps.append(best)
+    need = set()
+    for n, best in enumerate(deps):
+        need |= set(best.values())
+    for q in ENG_SEM:
+        need.add(max(n for n, o in enumerate(ops) if o["q"] == q and o["dma"] is None))
+    total = {}
+    for o in ops:
+        if o["dma"] not in (None, "remote"):
+            total[o["dma"]] = total.get(o["dma"], 0) + 16
+    count, mark, seen = {}, {}, {}
+
+    def wait(q, sem, v):
+        if seen.get((q, sem), 0) < v:
+            Q[q].wait_ge(T.sem[sem], v)
+            seen[(q, sem)] = v
+
+    for n, o in enumerate(ops):
+        for key, m in deps[n].items():
+            if ops[m]["dma"]:
+                wait(o["q"], key, total[key])
+            else:
+                wait(o["q"], ENG_SEM[key], mark[m])
+        for sem, v in o["waits"]:
+            wait(o["q"], sem, v)
+        ins = o["fn"]()
+        if o["dma"] is None:
+            if n in need:
+                count[o["q"]] = count.get(o["q"], 0) + 1
+                mark[n] = count[o["q"]]
+                ins.then_inc(T.sem[ENG_SEM[o["q"]]], 1)
+        elif o["dma"] != "remote":
+            ins.then_inc(T.sem[o["dma"]], 16)
+    for q in ENG_SEM:
+        wait("g", ENG_SEM[q], count[q])
+    for sem in total:
+        wait("g", sem, total[sem])
+    wait("g", "sent", nsent[0])

@@ -30,19 +30,21 @@ _b(BF, H, "covB")
 _b(F32, 512, "CAND", "MK", "SG")
 _b(F32, OG, "C", "YA", "YB")
 _b(F32, W, "YF", "DW")
-_b(BF, W, "MW", "HW", "TT")
-_b(BF, OG, "N0", "NA", "NB", "TD", "RW")
+_b(BF, W, "HW", "TT")
+_b(BF, 128, "NEG")
+_b(BF, OG, "N0", "NA", "NB", "TD", "RW", "RX")
 _b(BF, 688, "TL")
 _b(BF, 708, "ZB")
 _b(F32, E, "IO", "GA", "YS")
 _b(BF, E, "EQ", "EQ2", "V", "CUT")
-_b(BF, 144, "ONE")
-_b(F32, 128, "tmp3")
+_b(BF, 512, "ONE")
+_b(F32, 128, "tmp3", "IDF")
+_b(F16, 128, "IDH")
 _b(BF, 4 * W, "SW")
 _b(F32, LW + 7, "LWN")
 _b(BF, LW + 7, "GW", "MV")
 _b(U16, 128, "ptu", "LA", "LB", "bu", "bmu", "slu", "hiu", "hin")
-_b(U16, 48, "shu")
+_b(U16, 80, "shu")
 _b(BF, GH, "PS", "R1")
 _b(BF, 2 * GH, "tf")
 _b(F32, GH, "sa", "sb")
@@ -188,6 +190,7 @@ def rank_program(g, core, T, topo):
     iota(vw("selfI"), [[16, 128]], O, 0, False)
     asel(vw("Z0"), vw("ONE", 0, 144), [[-16, 9], [-BIG, 16]], ALU.is_ge, 16, 1)
     asel(vw("Z1"), vw("Z0"), [[16, 9], [0, 16]], ALU.is_ge, -1, -1)
+    asel(vw("IDB"), vw("ONE", 0, 128), [[-1, 128]], ALU.is_equal, 0, 1)
     iota(vw("IO"), [[1, E]], O, 0, True)
     iota(vw("TD"), [[16, OG // 16], [0, 16]], 0, 0, True)
     iota(vw("TL"), [[0, 43], [1, 16]], 0, 0, True)
@@ -196,8 +199,9 @@ def rank_program(g, core, T, topo):
             [vw("TD", 688 * k, 688 * k + 688)], [vw("TL")])
     asel(vw("ZD"), vw("Z0"), [[16, 9], [0, 16]], ALU.is_ge, -15, -1)
     ms(vw("ZB"), 0.0)
+    ms(vw("ONE", 144, 512), 1.0)
     ms(vw("C", 0, O), -4096.0)
-    for name in ("YA", "YB", "YF", "DW", "MW", "HW", "N0", "NA", "NB"):
+    for name in ("YA", "YB", "YF", "DW", "TT", "HW", "N0", "NA", "NB"):
         ms(vw(name, 0, O), 0.0)
     for name in ("LWN", "GW", "MV"):
         ms(vw(name), 0.0)
@@ -223,30 +227,44 @@ def rank_program(g, core, T, topo):
             mm(vw(PA[2], 64 * s, 64 * s + 64), vw("FF", 128 * k, 128 * k + 128), vw("curB", par, 127 + par, 2), par == 0, par == 1)
     for s in range(2):
         for i in range(4):
-            act(vw("CAND", 128 * i + 64 * s, 128 * i + 64 * s + 64), vw(PA[s], 64 * i, 64 * i + 64), AF.Identity, bias=float(1024 + O))
-    ts(vw("selfI"), vw("selfI"), vw("colF", 0, 1), ALU.add)
+            act(vw("CAND", 128 * i + 64 * s, 128 * i + 64 * s + 64), vw(PA[s], 64 * i, 64 * i + 64), AF.Identity, bias=float(O))
+    for h in range(2):
+        act(vw("C", O + H * h, O + H * h + H), vw("covB"), AF.Identity, bias=-8192.0)
+    act(vw("NEG"), vw("IDB"), scale=-128.0)
+    ts(vw("shH"), vw("shI"), 1, ALU.arith_shift_right)
+    ts(vw("shB"), vw("shI"), 1024.0, ALU.mult)
+    ts(vw("shA"), vw("shH"), -2047.0, ALU.mult, float(O), ALU.add)
     cp(vw("cF"), vw(PA[2], 0, 128))
-    cp(vw("colP", 0, 1), vw("ID4", 0, 1))
 
     def nxt_a(shift):
         for i in range(4):
-            ts(vw("MK", 128 * i, 128 * i + 128), vw("cF"), float((i - shift) % 4), ALU.is_equal)
+            if shift:
+                act(vw("MK", 128 * i, 128 * i + 128), vw("cF"), AF.Square, bias=-float((i - shift) % 4))
+            else:
+                ts(vw("MK", 128 * i, 128 * i + 128), vw("cF"), float(i), ALU.is_equal)
         if shift:
-            ts(vw("dc"), vw("MK", 0, 128), -4.0, ALU.mult, 1.0, ALU.add)
+            act(vw("MK"), vw("MK"), AF.Relu, bias=1.0, scale=-1.0)
+            act(vw("dc"), vw("MK", 0, 128), AF.Identity, bias=1.0, scale=-4.0)
 
     def nxt_b():
-        tt(vw("MK"), vw("MK"), vw("CAND"), ALU.mult)
+        tt(vw("uh"), vw("MK"), vw("CAND"), ALU.mult)
 
-    def nxt_c(k):
-        tt(vw("MK", 0, 256), vw("MK", 0, 256), vw("MK", 256, 512), ALU.add)
-        tt(vw("bn%d" % k), vw("MK", 0, 128), vw("MK", 128, 256), ALU.add)
+    def nxt_c(k, bank):
+        for i in range(4):
+            mm(vw(bank, 0, 128), vw("IDH"), vw("uh", 128 * i, 128 * i + 128), i == 0, i == 3)
+        ts(vw("bn%d" % k), vw(bank, 0, 128), 1024.0, ALU.add)
 
-    def nxt_d(k):
+    def nxt_d(k, part):
         bn = vw("bn%d" % k)
-        tt(vw("tmp3"), bn, vw("selfI"), ALU.not_equal)
-        ts(vw("lI"), bn, 15, ALU.bitwise_and)
-        ts(vw("hin"), bn, 1.0 / 16, ALU.mult, -0.46875, ALU.add)
-        tt(vw("LWN", 1, 129), bn, vw("tmp3"), ALU.mult)
+        if part == 1:
+            tt(vw("tmp3"), bn, vw("selfI"), ALU.not_equal)
+            ts(vw("hin"), bn, 1.0 / 16, ALU.mult, -0.46875, ALU.add)
+        elif part == 2:
+            tt(vw("LWN", 1, 129), bn, vw("tmp3"), ALU.mult)
+        else:
+            ts(vw("lI"), bn, 15, ALU.bitwise_and)
+
+    def nxt_e(k):
         ts(vw("xe"), vw("lI"), -LN2, ALU.mult, 15 * LN2, ALU.add)
         act(vw("P2n%d" % k), vw("xe"), AF.Exp)
 
@@ -269,18 +287,24 @@ def rank_program(g, core, T, topo):
             conv(vw(bank, 64 * h, 64 * h + 64), "ZP", "EQ", H * h, 64)
 
     nxt_a(0)
-    ts(vw("ZP"), vw("Z1"), vw("colP", 0, 1), ALU.mult)
+    cp(vw("IDH"), vw("IDB"))
     nxt_b()
-    nxt_c(1)
-    nxt_d(1)
-    mutual_gather(0, 1)
-    mutual_conv(PA[3])
-    for h in range(2):
-        act(vw("C", O + H * h, O + H * h + H), vw("covB"), AF.Identity, bias=-8192.0)
-    ts(vw("shH"), vw("shI"), 1, ALU.arith_shift_right)
-    ts(vw("shB"), vw("shI"), 1024.0, ALU.mult)
-    ts(vw("shA"), vw("shH"), -2047.0, ALU.mult, float(O), ALU.add)
+    ts(vw("selfI"), vw("selfI"), vw("colF", 0, 1), ALU.add)
+    cp(vw("colP", 0, 1), vw("ID4", 0, 1))
     tt(vw("shA"), vw("shA"), vw("shB"), ALU.add)
+    nxt_c(1, PA[2])
+    ts(vw("ZP"), vw("Z1"), vw("colP", 0, 1), ALU.mult)
+    nxt_d(1, 1)
+    nxt_d(1, 2)
+    mutual_gather(0)
+    nxt_d(1, 3)
+    mutual_gather(1)
+    mutual_conv(PA[3])
+    nxt_e(1)
+    ts(vw("shB"), vw("shA"), float(O + H), ALU.is_ge, -2.0 * H, ALU.mult)
+    cp(vw("shu", 0, 16), vw("shA"))
+    tt(vw("shB"), vw("shB"), vw("shA"), ALU.add)
+    ts(vw("shu", 32, 48), vw("shB"), float(H), ALU.add)
     bit(PA[3], vw("P2n1"))
     tt(vw("pt"), vw("bitI"), vw("bn1"), ALU.mult)
     cp(vw("ptu"), vw("pt"))
@@ -288,9 +312,10 @@ def rank_program(g, core, T, topo):
         dma("s", lambda k=k: T.SW[:, 708 * k:708 * k + 708], lambda: T.ZB[:, :], "ldz", [vw("SW", 708 * k, 708 * k + 708)], [vw("ZB")])
     for k in range(3):
         dma("s", lambda k=k: T.RW[:, 688 * k:688 * k + 688], lambda: T.ZB[:, 0:688], "ldz", [vw("RW", 688 * k, 688 * k + 688)], [vw("ZB")])
+        dma("s", lambda k=k: T.RX[:, 688 * k:688 * k + 688], lambda: T.ZB[:, 0:688], "ldz", [vw("RX", 688 * k, 688 * k + 688)], [vw("ZB")])
     asel(vw("SHM", 0, 96), vw("ONE", 0, 96), [[-1, 96]], ALU.is_equal, -32, 1)
     asel(vw("SHM", 96, 128), vw("ONE", 0, 32), [[-1, 32]], ALU.is_equal, 0, 1)
-    asel(vw("IDB"), vw("ONE", 0, 128), [[-1, 128]], ALU.is_equal, 0, 1)
+    asel(vw("IDF"), vw("ONE", 0, 128), [[-1, 128]], ALU.is_equal, 0, 1)
     asel(vw("SHP", 0, 32), vw("ONE", 0, 32), [[-16, 2], [BIG, 16]], ALU.is_equal, -96, 1)
     asel(vw("SHP", 32, 128), vw("ONE", 0, 96), [[-16, 6], [BIG, 16]], ALU.is_equal, 0, 1)
     for s in range(2):
@@ -307,11 +332,6 @@ def rank_program(g, core, T, topo):
         first = lambda h: vw("ptu", 64 * (1 - h), 64 * (1 - h) + 64)
         cp(half("N0", 0), (vw("TD"), first(0)))
         act(half("N0", 1), (vw("TD"), first(1)))
-        if r == 0:
-            ts(vw("shB"), vw("shA"), float(O + H), ALU.is_ge, -2.0 * H, ALU.mult)
-            cp(vw("shu", 0, 16), vw("shA"))
-            tt(vw("shB"), vw("shB"), vw("shA"), ALU.add)
-            ts(vw("shu", 32, 48), vw("shB"), float(H), ALU.add)
         ys_ = ["C", "YA", "YB", "YA", "YB", "YA", "YF"]
         yc_ = [None, "GA", "YS", "GA", "YS", "GA"]
         ns_ = ["N0", "NA", "NB", "NA", "NB", "NA"]
@@ -336,50 +356,59 @@ def rank_program(g, core, T, topo):
         def twin_a(k, h):
             act(vw(yc_[k], H * h + CG, H * h + H), vw(ys_[k], O + H * h + CG, O + H * h + H))
 
-        for k in range(1, 7):
-            if k < 6:
-                hop(k, 0)
-            else:
-                act(vw("PS"), (vw("N0"), vw("shu", 32, 48)))
-                conv(vw(PA[0], 0, 16), "ZD", "PS", 0, 16)
+        for k in range(1, 6):
+            hop(k, 0)
             if k > 1:
                 twin_a(k - 1, 1)
             add(k, 0)
             if k > 1:
                 take(k - 1, 1)
             add(k, 1)
-            if k < 6:
-                twin_g(k, 0)
-                hop(k, 1)
-                twin_a(k, 0)
-            else:
-                act(half("TT", 0), half("YF", 0), AF.Identity, bias=UNP, scale=-1.0 / 4096)
-                act(half("MW", 0), half("TT", 0), AF.Identity, bias=-128.0)
+            twin_g(k, 0)
+            hop(k, 1)
+            twin_a(k, 0)
             add(k, 2)
-            if k < 6:
-                take(k, 0)
-            else:
-                cp(vw("shu", 16, 32), vw(PA[0], 0, 16))
+            take(k, 0)
             add(k, 3)
-            if k < 6:
-                twin_g(k, 1)
+            twin_g(k, 1)
         SY, SD, SM, SH = "SY%d" % r, "SD%d" % r, "SM%d" % r, "SH%d" % r
-        cp(vw("SG", 0, GH), (vw("YF", 0, OG), vw("shu", 0, 16)))
-        mm(vw(PA[0], 0, GH), vw("SHM"), vw("SG", 0, GH), True, True)
-        cp(vw("SG", GH, 2 * GH), (vw("YF", 0, OG), vw("shu", 16, 32)))
-        mm(vw(PA[1], 0, GH), vw("SHM"), vw("SG", GH, 2 * GH), True, True)
-        cp(vw(SY), vw(PA[0], 0, GH))
         gz = lambda name, d: vw(name, OG + GH * (d - 1), OG + GH * d)
+        unp = lambda o, x: act(o, x, AF.Identity, bias=UNP, scale=-1.0 / 4096)
+        act(vw("R1"), (vw("NA"), vw("shu", 0, 16)))
+        conv(vw(PA[3], 0, 16), "ZD", "R1", 0, 16)
+        act(vw("sa"), (vw("YA"), vw("shu", 0, 16)))
+        twin_a(5, 1)
+        act(vw("PS"), (vw("N0"), vw("shu", 32, 48)))
+        conv(vw(PA[1], 0, 16), "ZD", "PS", 0, 16)
+        add(6, 0)
+        take(5, 1)
+        add(6, 1)
+        cp(vw("shu", 48, 64), vw(PA[3], 0, 16))
+        tt(vw("SG", 0, GH), (vw("YA"), vw("shu", 48, 64)), vw("sa"), ALU.add)
+        mm(vw(PA[2], 0, GH), vw("SHM"), vw("SG", 0, GH), True, True)
+        unp(half("TT", 0), half("YF", 0))
+        act(vw(SY), vw(PA[2], 0, GH))
         send([(d, vw(SY), gz("YF", d)) for d in range(1, N)], "ay%d" % r)
-        act(half("TT", 1), half("YF", 1), AF.Identity, bias=UNP, scale=-1.0 / 4096)
-        act(vw("tf", 0, GH), vw(SY), AF.Identity, bias=UNP, scale=-1.0 / 4096)
-        act(vw("tf", GH, 2 * GH), vw(PA[1], 0, GH), AF.Identity, bias=UNP, scale=-1.0 / 4096)
+        unp(vw("tf", 0, GH), vw(SY))
+        add(6, 2)
+        cp(vw("shu", 16, 32), vw(PA[1], 0, 16))
+        add(6, 3)
+
+        def mass(bank, q, one, neg):
+            mm(vw(bank), vw(neg), vw("ONE"), True, False)
+            mm(vw(bank), vw(one), ch("TT", q), False, True)
+        for q in (0, 1):
+            mm(vw(PB[q]), vw("IDF"), ch("YF", q), True, True)
+        cp(vw("SG", GH, 2 * GH), (vw("YF", 0, OG), vw("shu", 16, 32)))
+        mm(vw(PA[3], 0, GH), vw("SHM"), vw("SG", GH, 2 * GH), True, True)
+        unp(half("TT", 1), half("YF", 1))
+        unp(vw("tf", GH, 2 * GH), vw(PA[3], 0, GH))
         act(vw(SM), vw("tf"), AF.Identity, bias=-128.0)
-        send([(d, vw(SM, 0, GH), gz("MW", d)) for d in range(1, N)] + [(d, vw(SM, GH, 2 * GH), gz("HW", d)) for d in range(1, N)],
-             "am%d" % r)
-        act(half("MW", 1), half("TT", 1), AF.Identity, bias=-128.0)
-        for q in range(4):
-            act(vw(PB[q]), ch("YF", q))
+        send([(d, vw(SM, GH, 2 * GH), gz("HW", d)) for d in range(1, N)], "am%d" % r)
+        for q in (0, 1):
+            mass(PA[q], q, "IDB", "NEG")
+        for q in (2, 3):
+            mm(vw(PB[q]), vw("IDF"), ch("YF", q), True, True)
         if r == 0:
             cp(vw("bF"), vw("bn1"))
         else:
@@ -388,20 +417,22 @@ def rank_program(g, core, T, topo):
             tt(vw("bF"), vw("tmp"), vw("stayb"), ALU.add)
             tt(vw("cF"), vw("cF"), vw("tmp2"), ALU.add)
         cp(vw("bu"), vw("bF"))
-        tt(vw("sa"), vw(SM, 0, GH), vw(PA[1], 0, GH), ALU.mult)
-        tt(vw("sb"), vw(SY), vw(SM, GH, 2 * GH), ALU.mult)
-        for q in (2, 3, 0, 1):
-            mm(vw(PA[q]), vw("IDB"), ch("MW", q), True, True)
         tt(vw("tmp"), vw("bF"), vw("pt"), ALU.subtract)
-        tt(vw(SD), vw("sa"), vw("sb"), ALU.subtract)
-        send([(d, vw(SD), gz("DW", d)) for d in range(1, N)], "ad%d" % r)
         ts(vw("tmp2"), vw("cF"), float(W), ALU.mult)
         cp(vw("bmu"), vw("tmp"))
         tt(vw("tmp2"), vw("tmp2"), vw("bF"), ALU.add)
         if not last:
             nxt_a(1)
+        tt(vw("sb"), vw(SM, GH, 2 * GH), vw(PA[2], 0, GH), ALU.mult)
+        tt(vw(PA[3], 0, GH), vw(SM, 0, GH), vw(PA[3], 0, GH), ALU.mult)
         cp(vw("slu"), vw("tmp2"))
-        if r:
+        tt(vw(SD), vw("sb"), vw(PA[3], 0, GH), ALU.subtract)
+        send([(d, vw(SD), gz("DW", d)) for d in range(1, N)], "ad%d" % r)
+        for q in (2, 3):
+            mass(PA[q], q, "IDB", "NEG")
+        if r == 0:
+            cp(vw("P2"), vw("P2n1"))
+        else:
             tt(vw("dP"), vw("P2n%d" % kc), vw("P2"), ALU.subtract)
         wy, wd, wm = [[("%s%d" % (x, r), arrivals())] for x in ("ay", "ad", "am")]
         def f_a(q):
@@ -409,23 +440,26 @@ def rank_program(g, core, T, topo):
             tt(ch("YA", q), ch("GA", q, 0), vw(PA[q]), ALU.mult)
 
         def f_b(q):
-            act(ch("HW", q), (vw("MW"), lb("bu", q)), waits=wm)
+            act(ch("HW", q), (vw("TT"), lb("bu", q)), AF.Identity, bias=-128.0)
             tt(vw(PB[q]), ch("HW", q), vw(PB[q]), ALU.mult)
+
+        def f_c(q):
             tt(ch("DW", q), ch("YA", q), vw(PB[q]), ALU.subtract)
-        if not last:
-            nxt_b()
-        f_a(0); f_a(1); f_b(0); f_b(1); f_a(2); f_b(2); f_a(3); f_b(3)
+        ts(vw("TT", OG, W), vw("YF", OG, W), -1.0 / 4096, ALU.mult, UNP, ALU.add, waits=wy)
+        f_a(0); f_a(1); f_b(0); f_c(0); f_b(1); f_c(1); f_a(2); f_b(2); f_a(3); f_c(2); f_b(3); f_c(3)
 
         def s_0(q):
             act(vw(PB[q]), ch("DW", q), AF.Abs)
 
         def s_a(q):
             act(ch("GA", q, 0), (vw("DW"), lb("bmu", q)), AF.Abs, waits=wd)
-            act(ch("EQ", q, 0), (vw("HW"), lb("bmu", q)))
+            act(ch("EQ", q, 0), (vw("HW"), lb("bmu", q)), waits=wm)
 
         def s_b(q):
             tt(ch("YB", q), ch("GA", q, 0), vw(PA[q]), ALU.mult)
             tt(vw(PB[q]), ch("EQ", q, 0), vw(PB[q]), ALU.mult)
+
+        def s_c(q):
             tt(ch("V", q, 0), ch("YB", q), vw(PB[q]), ALU.is_gt)
             mm(vw(PB[q]), vw("Z1", 16, 144), ch("V", q, 0), True, True)
 
@@ -434,61 +468,83 @@ def rank_program(g, core, T, topo):
 
         def s_e(q):
             cp((vw("SW"), lb("slu", q)), ch("CUT", q, 0))
-        s_0(0); s_0(1)
+        s_0(0); s_0(1); s_0(2)
         if not last:
-            nxt_c(kn)
-        s_a(0); s_b(0); s_a(1); s_d(0); s_b(1); s_0(2); s_a(2); s_e(0); s_d(1); s_b(2); s_0(3); s_a(3)
-        s_e(1); s_d(2); s_b(3); s_d(3); s_e(2); s_e(3)
+            nxt_b()
+        else:
+            ts(vw("ID4"), vw("IDB"), 4096.0, ALU.mult)
+            ts(vw("NEG"), vw("IDB"), -128.0 * 4096, ALU.mult)
+            ts(vw("dc"), vw("cF"), 3.0, ALU.is_equal, -4.0, ALU.mult)
+            cp(vw("cB"), vw("cF"))
+            ts(vw("dc"), vw("dc"), 1.0, ALU.add)
+        s_a(0); s_b(0); s_c(0); s_a(1); s_d(0); s_b(1); s_c(1); s_a(2); s_e(0); s_d(1); s_b(2); s_0(3); s_a(3)
+        s_e(1); s_c(2); s_b(3); s_d(2); s_c(3); s_d(3); s_e(2); s_e(3)
+        if not last:
+            nxt_c(kn, PB[1])
+        else:
+            for q in range(4):
+                mass(PB[q], q, "ID4", "NEG")
         for d in range(1, N):
             for i in range(4):
                 lo = i * W + OG + GH * (d - 1)
                 mm(vw(PA[d - 1], 0, GH), vw("SHP"), vw("SW", lo, lo + GH), i == 0, i == 3)
-            o = vw(SH, GH * (d - 1), GH * d)
-            if d == 2:
-                act(o, vw(PA[d - 1], 0, GH), AF.Relu, bias=(1.0 - st) * st, scale=st)
-            else:
-                ts(o, vw(PA[d - 1], 0, GH), st, ALU.is_ge, st, ALU.mult)
+            if not last:
+                nxt_d(kn, d)
+            ts(vw(SH, GH * (d - 1), GH * d), vw(PA[d - 1], 0, GH), st, ALU.is_ge, float(8 ** r), ALU.mult)
         send([(N - d, vw(SH, GH * (d - 1), GH * d), vw("HR", GH * (d - 1), GH * d)) for d in range(1, N)], "ah%d" % r)
+        for j in range(16):
+            for i in range(4):
+                lo = i * W + O + j
+                mm(vw(PA[3], j, j + 113, 16), vw("SW", lo, lo + E - 15, 16), vw("Z1", 16, 129, 16), i == 0, i == 3)
+        ts(vw("hiu"), vw("pt"), 1.0 / 16, ALU.mult, -0.46875, ALU.add)
+        ts(vw("shB"), vw("shu", 16, 32), 0.0, ALU.is_equal)
+        if not last:
+            nxt_e(kn)
+        cp(vw("shH"), vw("shu", 16, 32))
+        tt(vw("shB"), vw("shB"), vw("shA"), ALU.mult)
+        act(vw("xc"), vw("pt"), AF.Relu, bias=2.0, scale=-2.0)
+        act(vw("curB"), vw(PA[3], 0, 128), AF.Sign, bias=0.5 - st)
+        mm(vw(PA[1], 0, 128), vw("IDB"), vw("xc"), True, False)
+        mm(vw(PA[1], 0, 128), vw("curB"), vw("IDB"), False, True)
+        act(vw("unl"), vw(PA[1], 0, 128), AF.Sign)
+        act(vw("GW", 1, 129), vw("unl"), AF.Relu)
         if last:
-            ts(vw("ID4"), vw("IDB"), 4096.0, ALU.mult)
             for q in range(4):
-                mm(vw(PB[q]), vw("ID4"), ch("MW", q), True, True)
                 lo = 2 * 512 * (q % 2) + 1 - q // 2
                 tt(vw("YS", lo, lo + 1023, 2), ch("YF", q), vw(PB[q]), ALU.add)
             dma("s", lambda: T.ys[:, :], lambda: T.YS[:, :], "sty", [], [vw("YS")])
-        for i in range(4):
-            conv(vw(PA[3], 0, 128), "Z1", "SW", i * W + O, 128, first=i == 0, last=False)
         if not last:
-            nxt_d(kn)
             mutual_gather(0, 1)
             mutual_conv(PB[0])
-        else:
-            ts(vw("dc"), vw("cF"), 3.0, ALU.is_equal, -4.0, ALU.mult)
-            cp(vw("cB"), vw("cF"))
-            ts(vw("dc"), vw("dc"), 1.0, ALU.add)
-        tt(vw("R1"), vw("HR", 0, GH), vw("HR", GH, 2 * GH), ALU.add, waits=[("ah%d" % r, arrivals())])
-        tt((vw("RW"), vw("shu", 0, 16)), vw("R1"), vw("HR", 2 * GH, 3 * GH), ALU.add)
-        conv(vw(PA[3], 0, 128), "Z1", "RW", O, 128, first=False, last=True)
-        ts(vw("hiu"), vw("pt"), 1.0 / 16, ALU.mult, -0.46875, ALU.add)
-        if r == 0:
-            cp(vw("P2"), vw("P2n1"))
-        else:
+        elif r:
             tt(vw("tmp"), vw("MV", 1, 129), vw("dP"), ALU.mult)
-        ts(vw("unl"), vw("pt"), 0.0, ALU.is_equal)
-        if r:
             tt(vw("P2"), vw("P2"), vw("tmp"), ALU.add)
-        ts(vw("GW", 1, 129), vw(PA[3], 0, 128), st, ALU.is_ge)
-        look("GW", "hiu", PA[0])
-        tt(vw("u0"), vw("GW", 1, 129), vw("unl"), ALU.max)
+        act(vw("EQ", 0, H), (vw("GW"), lists("hiu", 0)))
+        conv(vw(PA[0], 0, 64), "ZP", "EQ", 0, 64)
+        act(vw("EQ", H, E), (vw("GW"), lists("hiu", 1)))
+        act(vw("u0"), vw("GW", 1, 129), AF.Identity, bias=float(8 ** r), scale=-float(8 ** r))
+        tt(vw("shB"), vw("shB"), vw("shH"), ALU.add)
+        tt(vw("R1"), vw("HR", 0, GH), vw("HR", GH, 2 * GH), ALU.add, waits=[("ah%d" % r, arrivals())])
+        cp(vw("shu", 64, 80), vw("shB"))
+        tt((vw("RW"), vw("shu", 0, 16)), vw("R1"), vw("HR", 2 * GH, 3 * GH), ALU.add)
+        conv(vw(PA[2], 0, 128), "Z1", "RW", O, 128, first=True, last=False)
+        tt((vw("RX"), vw("shu", 64, 80)), vw("R1"), vw("HR", 2 * GH, 3 * GH), ALU.add)
+        conv(vw(PA[0], 64, 128), "ZP", "EQ", H, 64)
+        conv(vw(PA[2], 0, 128), "Z1", "RX", O, 128, first=False, last=True)
+        if r and not last:
+            tt(vw("tmp"), vw("MV", 1, 129), vw("dP"), ALU.mult)
         if not last:
             tt(vw("lI"), vw(PB[0], 0, 128), vw("P2n%d" % kn), ALU.mult)
-        tt(vw("tI"), vw(PA[0], 0, 128), vw("P2"), ALU.mult)
+        if r and not last:
+            tt(vw("P2"), vw("P2"), vw("tmp"), ALU.add)
         if not last:
             ts(vw("lI"), vw("lI"), 15, ALU.arith_shift_right, 1, ALU.bitwise_and)
-        ts(vw("bitI"), vw("tI"), 15, ALU.arith_shift_right, 1, ALU.bitwise_and)
+        tt(vw("tI"), vw(PA[0], 0, 128), vw("P2"), ALU.mult)
         if not last:
             tt(vw("P2q"), vw("lI"), vw("P2n%d" % kn), ALU.mult)
-        tt(vw("MV", 1, 129), vw("bitI"), vw("u0"), ALU.max)
+        ts(vw("bitI"), vw("tI"), 15 - 3 * r, ALU.arith_shift_right, 8 ** r, ALU.bitwise_and)
+        tt(vw("u0"), vw("u0"), vw("bitI"), ALU.subtract)
+        tt(vw("MV", 1, 129), vw(PA[2], 0, 128), vw("u0"), ALU.is_ge)
         if not last:
             look("MV", "hin", PA[1])
             ts(vw("nm"), vw("MV", 1, 129), -1.0, ALU.mult, 1.0, ALU.add)

import math
from concourse.bass import DstId, RemoteDMATransfer
from concourse.mybir import AluOpType as ALU, ActivationFunctionType as AF

N, RO = 4, 4
E, H, GH = 2048, 1024, 256
O = 16
OG = O + E
W = OG + (N - 1) * GH
LW = W // 16 + 1
F32, BF, I32, U16, F16 = "float32", "bfloat16", "int32", "uint16", "float16"

SCRATCH = {}
def _b(dtype, cols, *names):
    for n in names:
        SCRATCH[n] = ("sbuf", [128, cols], dtype)
_b(I32, 512, "candI", "hI")
_b(I32, 128, "curI", "tI", "bitI", "lI", "selfI", "bn0", "bn1")
_b(I32, 16, "shI", "shH")
_b(I32, 8, "colI")
_b(F32, 8, "colF", "colP")
_b(F32, 16, "shA", "shB")
_b(F16, 512, "c1h", "h1h", "uh", "FA", "FB", "FC")
_b(BF, 128, "curB", "IDB", "ID4", "SHP", "xc", "cB")
_b(BF, 512, "FF", "FI")
_b(F32, 128, "SHM", "cF", "bF", "pt", "unl", "u0", "nm", "stayb", "tmp", "tmp2", "dc", "xe", "ycs", "P2", "P2q", "P2m", "dP")
_b(BF, 128, "P2n0", "P2n1")
_b(BF, 144, "Z1", "ZP", "ZD", "Z0")
_b(BF, H, "covB")
_b(F32, 512, "CAND", "MK", "SG")
_b(F32, OG, "C", "YA", "YB")
_b(F32, W, "YF", "DW")
_b(BF, W, "HW", "TT")
_b(BF, 128, "NEG")
_b(BF, OG, "N0", "NA", "NB", "TD", "RW", "RX")
_b(BF, 688, "TL")
_b(BF, 708, "ZB")
_b(F32, E, "IO", "GA", "YS")
_b(BF, E, "EQ", "EQ2", "V", "CUT")
_b(BF, 512, "ONE")
_b(F32, 128, "tmp3", "IDF")
_b(F16, 128, "IDH")
_b(BF, 4 * W, "SW")
_b(F32, LW + 7, "LWN")
_b(BF, LW + 7, "GW", "MV")
_b(U16, 128, "ptu", "LA", "LB", "bu", "bmu", "slu", "hiu", "hin")
_b(U16, 80, "shu")
_b(BF, GH, "PS", "R1")
_b(BF, 2 * GH, "tf")
_b(F32, GH, "sa", "sb")
_b(BF, 3 * GH, "HR")
for _r in range(RO):
    _b(F32, GH, "SY%d" % _r, "SD%d" % _r)
    _b(BF, 2 * GH, "SM%d" % _r)
    _b(BF, 3 * GH, "SH%d" % _r)
for _k in range(4):
    SCRATCH["PA%d" % _k] = ("psum", [128, 512], F32)
    SCRATCH["PB%d" % _k] = ("psum", [128, 512], F32)

SEMAPHORES = ["sv", "sa", "sp", "sg", "sent", "ldc", "ldu", "lds", "ldv", "ldt", "ldz", "sty", "stc"] + \
    ["%s%d" % (k, r) for k in ("ay", "ad", "am", "ah") for r in range(RO)]
ENG_SEM = {"v": "sv", "a": "sa", "p": "sp", "g": "sg"}
CG = 768


def rank_program(g, core, T, topo):
    rank = T.rank_of(core)
    if rank is None:
        return
    Q = {"v": g.vector, "a": g.scalar, "p": g.tensor, "g": g, "s": g.sync}
    ops = []

    def vw(name, lo=0, hi=None, step=1):
        return (name, lo, SCRATCH[name][1][1] if hi is None else hi, step)

    def ap(v):
        if len(v) == 2:
            return ap(v[0]).indirect(ap(v[1]))
        return T[v[0]][:, v[1]:v[2]] if v[3] == 1 else T[v[0]][:, v[1]:v[2]:v[3]]

    def parts(v):
        return [v[0], v[1]] if len(v) == 2 else [v]

    def isv(x):
        return isinstance(x, tuple)

    def val(x):
        return ap(x) if isv(x) else x

    def rec(q, fn, out, ins, waits=(), dma=None):
        rd, wr = [], []
        for v in ins:
            if isv(v):
                rd += parts(v)
        for v in out:
            if len(v) == 2:
                wr.append(v[0]); rd.append(v[1])
            else:
                wr.append(v)
        ops.append({"q": q, "fn": fn, "rd": rd, "wr": wr, "waits": list(waits), "dma": dma})

    def tt(out, a, b, op, waits=()):
        rec("v", lambda: g.vector.tensor_tensor(ap(out), ap(a), ap(b), op), [out], [a, b], waits)

    def ts(out, a, s1, op0, s2=None, op1=None, waits=()):
        if op1 is None:
            rec("v", lambda: g.vector.tensor_scalar(ap(out), ap(a), val(s1), None, op0), [out], [a, s1], waits)
        else:
            rec("v", lambda: g.vector.tensor_scalar(ap(out), ap(a), val(s1), val(s2), op0, op1), [out], [a, s1, s2], waits)

    def cp(out, a, waits=()):
        rec("v", lambda: g.vector.tensor_copy(ap(out), ap(a)), [out], [a], waits)

    def ms(out, c):
        rec("v", lambda: g.vector.memset(ap(out), c), [out], [])

    def act(out, a, f=AF.Copy, bias=None, scale=None, waits=()):
        kw = {}
        if bias is not None:
            kw["bias"] = bias
        if scale is not None:
            kw["scale"] = scale
        rec("a", lambda: g.scalar.activation(ap(out), ap(a), f, **kw), [out], [a], waits)

    def mm(out, l, r, st, sp):
        rec("p", lambda: g.tensor.matmul(ap(out), ap(l), ap(r), st, sp), [out], [l, r])

    def asel(out, a, pat, op, base, cm):
        rec("g", lambda: g.affine_select(ap(out), ap(a), pat, op, 0.0, base, cm), [out], [a])

    def iota(out, pat, base, cm, flt):
        if flt:
            rec("g", lambda: g.iota(ap(out), pat, base, cm, allow_small_or_imprecise_dtypes=True), [out], [])
        else:
            rec("g", lambda: g.iota(ap(out), pat, base, cm), [out], [])

    def dma(q, o, i, sem, out, ins):
        rec(q, lambda: Q[q].dma_start(o(), i()), out, ins, dma=sem)

    def conv(out, z, name, lo, n, first=True, last=True):
        for i in range(16):
            mm(out, vw(z, 16 - i, 144 - i), vw(name, lo + i, lo + i + 16 * (n - 1) + 1, 16), first and i == 0, last and i == 15)

    def peer(d):
        return T.cores[(rank + d) % N]
    free = {}
    order = sorted(range(1, N), key=lambda d: len(topo.engines(core, peer(d))))
    narrow = [d for d in order if len(topo.engines(core, peer(d))) == len(topo.engines(core, peer(order[0])))]
    used = []
    for d in order:
        left = [e for e in topo.engines(core, peer(d)) if e not in used]
        k = len(topo.engines(core, peer(d))) // len(narrow) if d in narrow else len(left)
        k = 1 << (k.bit_length() - 1)
        free[d] = left[:k]
        used += left[:k]
    nsent = [0]

    def arrivals():
        return sum(len(v) for v in free.values())

    def send(items, sem):
        def fn():
            tr = []
            share = len(items) // (N - 1)
            for j, (d, s, t) in enumerate(items):
                rid, pid = topo.addr(peer(d), core)
                mine = free[d][j // (N - 1)::share]
                tr.append(RemoteDMATransfer(dst_ids=[DstId(rid=rid, pnc=pid)], dma_engine_mask=sum(1 << e for e in mine),
                                            remote_sem=T.sem[sem], src=ap(s), dst=ap(t)))
            return g.remote_dma_fused(tr, local_sem=T.sem["sent"])
        rec("g", fn, [], [s for d, s, t in items], dma="remote")
        nsent[0] += arrivals()

    PA = ["PA%d" % k for k in range(4)]
    PB = ["PB%d" % k for k in range(4)]
    BIG = 1000
    LN2 = math.log(2.0)
    UNP = 128.4921875

    dma("s", lambda: T.candI[:, :], lambda: T.cand[:, :], "ldc", [vw("candI")], [])
    dma("a", lambda: T.curI[:, :], lambda: T.cur0[:, :], "ldu", [vw("curI")], [])
    dma("a", lambda: T.covB[:, :], lambda: T.cov[:, :], "ldv", [vw("covB")], [])
    dma("s", lambda: T.shI[:, :], lambda: T.shown[:, :], "lds", [vw("shI")], [])
    ms(vw("ONE", 0, 144), 1.0)
    for s in range(2):
        for par in range(2):
            k = 2 * s + par
            asel(vw("FF", 128 * k, 128 * k + 128), vw("ONE", 0, 128), [[-16, 8], [BIG, 2], [-2, 8]], ALU.is_equal, -s - BIG * par, 1)
    iota(vw("colI", 0, 1), [[0, 1]], 0, 1, False)
    iota(vw("selfI"), [[16, 128]], O, 0, False)
    asel(vw("Z0"), vw("ONE", 0, 144), [[-16, 9], [-BIG, 16]], ALU.is_ge, 16, 1)
    asel(vw("Z1"), vw("Z0"), [[16, 9], [0, 16]], ALU.is_ge, -1, -1)
    asel(vw("IDB"), vw("ONE", 0, 128), [[-1, 128]], ALU.is_equal, 0, 1)
    iota(vw("IO"), [[1, E]], O, 0, True)
    iota(vw("TD"), [[16, OG // 16], [0, 16]], 0, 0, True)
    iota(vw("TL"), [[0, 43], [1, 16]], 0, 0, True)
    for k in range(3):
        dma("s", lambda k=k: T.TD[1:128:16, 688 * k:688 * k + 688], lambda: T.TL[1:128:16, :], "ldt",
            [vw("TD", 688 * k, 688 * k + 688)], [vw("TL")])
    asel(vw("ZD"), vw("Z0"), [[16, 9], [0, 16]], ALU.is_ge, -15, -1)
    ms(vw("ZB"), 0.0)
    ms(vw("ONE", 144, 512), 1.0)
    ms(vw("C", 0, O), -4096.0)
    for name in ("YA", "YB", "YF", "DW", "TT", "HW", "N0", "NA", "NB"):
        ms(vw(name, 0, O), 0.0)
    for name in ("LWN", "GW", "MV"):
        ms(vw(name), 0.0)
    cp(vw("FC"), vw("FF"))
    ts(vw("colI", 1, 2), vw("colI", 0, 1), 15, ALU.bitwise_and)
    ts(vw("uh"), vw("candI"), -1024.0, ALU.add)
    cp(vw("colF", 0, 1), vw("colI", 1, 2))
    ts(vw("FA"), vw("FF"), 1023.0, ALU.mult)
    act(vw("ID4", 0, 1), vw("colF", 0, 1), AF.Exp, scale=LN2)
    ts(vw("c1h"), vw("candI"), 2047.0, ALU.min)
    ts(vw("hI"), vw("candI"), 1, ALU.arith_shift_right)
    ts(vw("FB"), vw("FF"), -2047.0, ALU.mult)
    ts(vw("h1h"), vw("hI"), 1023.0, ALU.min)
    cp(vw("curB"), vw("curI"))
    for n, (f, x) in enumerate((("FC", "uh"), ("FA", "c1h"), ("FB", "h1h"))):
        for s in range(2):
            for par in range(2):
                k = 2 * s + par
                mm(vw(PA[s], 0, 256), vw(f, 128 * k, 128 * k + 128), vw(x, par, 511 + par, 2), n + par == 0, n + par == 3)
    for s in range(2):
        for par in range(2):
            k = 2 * s + par
            mm(vw(PA[2], 64 * s, 64 * s + 64), vw("FF", 128 * k, 128 * k + 128), vw("curB", par, 127 + par, 2), par == 0, par == 1)
    for s in range(2):
        for i in range(4):
            act(vw("CAND", 128 * i + 64 * s, 128 * i + 64 * s + 64), vw(PA[s], 64 * i, 64 * i + 64), AF.Identity, bias=float(O))
    for h in range(2):
        act(vw("C", O + H * h, O + H * h + H), vw("covB"), AF.Identity, bias=-8192.0)
    act(vw("NEG"), vw("IDB"), scale=-128.0)
    ts(vw("shH"), vw("shI"), 1, ALU.arith_shift_right)
    ts(vw("shB"), vw("shI"), 1024.0, ALU.mult)
    ts(vw("shA"), vw("shH"), -2047.0, ALU.mult, float(O), ALU.add)
    cp(vw("cF"), vw(PA[2], 0, 128))

    def nxt_a(shift):
        for i in range(4):
            if shift:
                act(vw("MK", 128 * i, 128 * i + 128), vw("cF"), AF.Square, bias=-float((i - shift) % 4))
            else:
                ts(vw("MK", 128 * i, 128 * i + 128), vw("cF"), float(i), ALU.is_equal)
        if shift:
            act(vw("MK"), vw("MK"), AF.Relu, bias=1.0, scale=-1.0)
            act(vw("dc"), vw("MK", 0, 128), AF.Identity, bias=1.0, scale=-4.0)

    def nxt_b():
        tt(vw("uh"), vw("MK"), vw("CAND"), ALU.mult)

    def nxt_c(k, bank):
        for i in range(4):
            mm(vw(bank, 0, 128), vw("IDH"), vw("uh", 128 * i, 128 * i + 128), i == 0, i == 3)
        ts(vw("bn%d" % k), vw(bank, 0, 128), 1024.0, ALU.add)

    def nxt_d(k, part):
        bn = vw("bn%d" % k)
        if part == 1:
            tt(vw("tmp3"), bn, vw("selfI"), ALU.not_equal)
            ts(vw("hin"), bn, 1.0 / 16, ALU.mult, -0.46875, ALU.add)
        elif part == 2:
            tt(vw("LWN", 1, 129), bn, vw("tmp3"), ALU.mult)
        else:
            ts(vw("lI"), bn, 15, ALU.bitwise_and)

    def nxt_e(k):
        ts(vw("xe"), vw("lI"), -LN2, ALU.mult, 15 * LN2, ALU.add)
        act(vw("P2n%d" % k), vw("xe"), AF.Exp)

    def mutual_gather(*hs):
        for h in hs:
            tt(vw("EQ2", H * h, H * h + H), (vw("LWN"), vw("hin", 64 * h, 64 * h + 64)), vw("IO", H * h, H * h + H), ALU.is_equal)

    def mutual_conv(bank):
        for h in range(2):
            conv(vw(bank, 64 * h, 64 * h + 64), "ZP", "EQ2", H * h, 64)

    def bit(bank, p2):
        tt(vw("tI"), vw(bank, 0, 128), p2, ALU.mult)
        ts(vw("bitI"), vw("tI"), 15, ALU.arith_shift_right, 1, ALU.bitwise_and)

    def look(win, offs, bank):
        for h in range(2):
            cp(vw("EQ", H * h, H * h + 512), (vw(win), vw(offs, 64 * h, 64 * h + 32)))
            act(vw("EQ", H * h + 512, H * h + H), (vw(win), vw(offs, 64 * h + 32, 64 * h + 64)))
            conv(vw(bank, 64 * h, 64 * h + 64), "ZP", "EQ", H * h, 64)

    nxt_a(0)
    cp(vw("IDH"), vw("IDB"))
    nxt_b()
    ts(vw("selfI"), vw("selfI"), vw("colF", 0, 1), ALU.add)
    cp(vw("colP", 0, 1), vw("ID4", 0, 1))
    tt(vw("shA"), vw("shA"), vw("shB"), ALU.add)
    nxt_c(1, PA[2])
    ts(vw("ZP"), vw("Z1"), vw("colP", 0, 1), ALU.mult)
    nxt_d(1, 1)
    nxt_d(1, 2)
    mutual_gather(0)
    nxt_d(1, 3)
    mutual_gather(1)
    mutual_conv(PA[3])
    nxt_e(1)
    ts(vw("shB"), vw("shA"), float(O + H), ALU.is_ge, -2.0 * H, ALU.mult)
    cp(vw("shu", 0, 16), vw("shA"))
    tt(vw("shB"), vw("shB"), vw("shA"), ALU.add)
    ts(vw("shu", 32, 48), vw("shB"), float(H), ALU.add)
    bit(PA[3], vw("P2n1"))
    tt(vw("pt"), vw("bitI"), vw("bn1"), ALU.mult)
    cp(vw("ptu"), vw("pt"))
    for k in range(16):
        dma("s", lambda k=k: T.SW[:, 708 * k:708 * k + 708], lambda: T.ZB[:, :], "ldz", [vw("SW", 708 * k, 708 * k + 708)], [vw("ZB")])
    for k in range(3):
        dma("s", lambda k=k: T.RW[:, 688 * k:688 * k + 688], lambda: T.ZB[:, 0:688], "ldz", [vw("RW", 688 * k, 688 * k + 688)], [vw("ZB")])
        dma("s", lambda k=k: T.RX[:, 688 * k:688 * k + 688], lambda: T.ZB[:, 0:688], "ldz", [vw("RX", 688 * k, 688 * k + 688)], [vw("ZB")])
    asel(vw("SHM", 0, 96), vw("ONE", 0, 96), [[-1, 96]], ALU.is_equal, -32, 1)
    asel(vw("SHM", 96, 128), vw("ONE", 0, 32), [[-1, 32]], ALU.is_equal, 0, 1)
    asel(vw("IDF"), vw("ONE", 0, 128), [[-1, 128]], ALU.is_equal, 0, 1)
    asel(vw("SHP", 0, 32), vw("ONE", 0, 32), [[-16, 2], [BIG, 16]], ALU.is_equal, -96, 1)
    asel(vw("SHP", 32, 128), vw("ONE", 0, 96), [[-16, 6], [BIG, 16]], ALU.is_equal, 0, 1)
    for s in range(2):
        for par in range(2):
            k = 2 * s + par
            asel(vw("FI", 128 * k, 128 * k + 128), vw("ONE", 0, 128), [[-16, 8], [-1, 8], [BIG, 2]], ALU.is_equal, -8 * par - BIG * s, 1)

    for r in range(RO):
        st = float(64 ** r)
        last = r == RO - 1
        kc, kn = (r + 1) % 2, r % 2
        half = lambda name, h: vw(name, O + H * h, O + H * h + H)
        lists = lambda name, h: vw(name, 64 * h, 64 * h + 64)
        first = lambda h: vw("ptu", 64 * (1 - h), 64 * (1 - h) + 64)
        cp(half("N0", 0), (vw("TD"), first(0)))
        act(half("N0", 1), (vw("TD"), first(1)))
        ys_ = ["C", "YA", "YB", "YA", "YB", "YA", "YF"]
        yc_ = [None, "GA", "YS", "GA", "YS", "GA"]
        ns_ = ["N0", "NA", "NB", "NA", "NB", "NA"]
        ls_ = [None, "LA", "LB", "LA", "LB", "LA"]
        ch = lambda name, q, o=O: vw(name, o + 512 * q, o + 512 * q + 512)
        lb = lambda name, q: vw(name, 32 * q, 32 * q + 32)

        def add(k, q):
            own = ch("covB", q % 2, 0) if k == 1 else ch(yc_[k - 1], q, 0)
            tt(ch(ys_[k], q), (vw(ys_[k - 1], 0, OG), lb("ptu", q ^ 2) if k == 1 else lb(ls_[k - 1], q)), own, ALU.add)

        def hop(k, h):
            act(half(ns_[k], h), (vw(ns_[k - 1]), first(h) if k == 1 else lists(ls_[k - 1], h)))
            conv(vw(PB[2 * (k % 2) + h], 0, 64), "ZD", ns_[k], O + H * h, 64)

        def take(k, h):
            cp(lists(ls_[k], h), vw(PB[2 * (k % 2) + h], 0, 64))

        def twin_g(k, h):
            asel(vw(yc_[k], H * h, H * h + CG), vw(ys_[k], O + H * h, O + H * h + CG), [[0, CG]], ALU.is_ge, 0, 0)

        def twin_a(k, h):
            act(vw(yc_[k], H * h + CG, H * h + H), vw(ys_[k], O + H * h + CG, O + H * h + H))

        for k in range(1, 6):
            hop(k, 0)
            if k > 1:
                twin_a(k - 1, 1)
            add(k, 0)
            if k > 1:
                take(k - 1, 1)
            add(k, 1)
            twin_g(k, 0)
            hop(k, 1)
            twin_a(k, 0)
            add(k, 2)
            take(k, 0)
            add(k, 3)
            twin_g(k, 1)
        SY, SD, SM, SH = "SY%d" % r, "SD%d" % r, "SM%d" % r, "SH%d" % r
        gz = lambda name, d: vw(name, OG + GH * (d - 1), OG + GH * d)
        unp = lambda o, x: act(o, x, AF.Identity, bias=UNP, scale=-1.0 / 4096)
        act(vw("R1"), (vw("NA"), vw("shu", 0, 16)))
        conv(vw(PA[3], 0, 16), "ZD", "R1", 0, 16)
        act(vw("sa"), (vw("YA"), vw("shu", 0, 16)))
        twin_a(5, 1)
        act(vw("PS"), (vw("N0"), vw("shu", 32, 48)))
        conv(vw(PA[1], 0, 16), "ZD", "PS", 0, 16)
        add(6, 0)
        take(5, 1)
        add(6, 1)
        cp(vw("shu", 48, 64), vw(PA[3], 0, 16))
        tt(vw("SG", 0, GH), (vw("YA"), vw("shu", 48, 64)), vw("sa"), ALU.add)
        mm(vw(PA[2], 0, GH), vw("SHM"), vw("SG", 0, GH), True, True)
        unp(half("TT", 0), half("YF", 0))
        act(vw(SY), vw(PA[2], 0, GH))
        send([(d, vw(SY), gz("YF", d)) for d in range(1, N)], "ay%d" % r)
        unp(vw("tf", 0, GH), vw(SY))
        add(6, 2)
        cp(vw("shu", 16, 32), vw(PA[1], 0, 16))
        add(6, 3)

        def mass(bank, q, one, neg):
            mm(vw(bank), vw(neg), vw("ONE"), True, False)
            mm(vw(bank), vw(one), ch("TT", q), False, True)
        for q in (0, 1):
            mm(vw(PB[q]), vw("IDF"), ch("YF", q), True, True)
        cp(vw("SG", GH, 2 * GH), (vw("YF", 0, OG), vw("shu", 16, 32)))
        mm(vw(PA[3], 0, GH), vw("SHM"), vw("SG", GH, 2 * GH), True, True)
        unp(half("TT", 1), half("YF", 1))
        unp(vw("tf", GH, 2 * GH), vw(PA[3], 0, GH))
        act(vw(SM), vw("tf"), AF.Identity, bias=-128.0)
        send([(d, vw(SM, GH, 2 * GH), gz("HW", d)) for d in range(1, N)], "am%d" % r)
        for q in (0, 1):
            mass(PA[q], q, "IDB", "NEG")
        for q in (2, 3):
            mm(vw(PB[q]), vw("IDF"), ch("YF", q), True, True)
        if r == 0:
            cp(vw("bF"), vw("bn1"))
        else:
            tt(vw("tmp"), vw("MV", 1, 129), vw("bn%d" % kc), ALU.mult)
            tt(vw("tmp2"), vw("MV", 1, 129), vw("dc"), ALU.mult)
            tt(vw("bF"), vw("tmp"), vw("stayb"), ALU.add)
            tt(vw("cF"), vw("cF"), vw("tmp2"), ALU.add)
        cp(vw("bu"), vw("bF"))
        tt(vw("tmp"), vw("bF"), vw("pt"), ALU.subtract)
        ts(vw("tmp2"), vw("cF"), float(W), ALU.mult)
        cp(vw("bmu"), vw("tmp"))
        tt(vw("tmp2"), vw("tmp2"), vw("bF"), ALU.add)
        if not last:
            nxt_a(1)
        tt(vw("sb"), vw(SM, GH, 2 * GH), vw(PA[2], 0, GH), ALU.mult)
        tt(vw(PA[3], 0, GH), vw(SM, 0, GH), vw(PA[3], 0, GH), ALU.mult)
        cp(vw("slu"), vw("tmp2"))
        tt(vw(SD), vw("sb"), vw(PA[3], 0, GH), ALU.subtract)
        send([(d, vw(SD), gz("DW", d)) for d in range(1, N)], "ad%d" % r)
        for q in (2, 3):
            mass(PA[q], q, "IDB", "NEG")
        if r == 0:
            cp(vw("P2"), vw("P2n1"))
        else:
            tt(vw("dP"), vw("P2n%d" % kc), vw("P2"), ALU.subtract)
        wy, wd, wm = [[("%s%d" % (x, r), arrivals())] for x in ("ay", "ad", "am")]
        def f_a(q):
            act(ch("GA", q, 0), (vw("YF"), lb("bu", q)), waits=wy)
            tt(ch("YA", q), ch("GA", q, 0), vw(PA[q]), ALU.mult)

        def f_b(q):
            act(ch("HW", q), (vw("TT"), lb("bu", q)), AF.Identity, bias=-128.0)
            tt(vw(PB[q]), ch("HW", q), vw(PB[q]), ALU.mult)

        def f_c(q):
            tt(ch("DW", q), ch("YA", q), vw(PB[q]), ALU.subtract)
        ts(vw("TT", OG, W), vw("YF", OG, W), -1.0 / 4096, ALU.mult, UNP, ALU.add, waits=wy)
        f_a(0); f_a(1); f_b(0); f_c(0); f_b(1); f_c(1); f_a(2); f_b(2); f_a(3); f_c(2); f_b(3); f_c(3)

        def s_0(q):
            act(vw(PB[q]), ch("DW", q), AF.Abs)

        def s_a(q):
            act(ch("GA", q, 0), (vw("DW"), lb("bmu", q)), AF.Abs, waits=wd)
            act(ch("EQ", q, 0), (vw("HW"), lb("bmu", q)), waits=wm)

        def s_b(q):
            tt(ch("YB", q), ch("GA", q, 0), vw(PA[q]), ALU.mult)
            tt(vw(PB[q]), ch("EQ", q, 0), vw(PB[q]), ALU.mult)

        def s_c(q):
            tt(ch("V", q, 0), ch("YB", q), vw(PB[q]), ALU.is_gt)
            mm(vw(PB[q]), vw("Z1", 16, 144), ch("V", q, 0), True, True)

        def s_d(q):
            act(ch("CUT", q, 0), vw(PB[q]), AF.Relu, bias=-8.0 * st, scale=st)

        def s_e(q):
            cp((vw("SW"), lb("slu", q)), ch("CUT", q, 0))
        s_0(0); s_0(1); s_0(2)
        if not last:
            nxt_b()
        else:
            ts(vw("ID4"), vw("IDB"), 4096.0, ALU.mult)
            ts(vw("NEG"), vw("IDB"), -128.0 * 4096, ALU.mult)
            ts(vw("dc"), vw("cF"), 3.0, ALU.is_equal, -4.0, ALU.mult)
            cp(vw("cB"), vw("cF"))
            ts(vw("dc"), vw("dc"), 1.0, ALU.add)
        s_a(0); s_b(0); s_c(0); s_a(1); s_d(0); s_b(1); s_c(1); s_a(2); s_e(0); s_d(1); s_b(2); s_0(3); s_a(3)
        s_e(1); s_c(2); s_b(3); s_d(2); s_c(3); s_d(3); s_e(2); s_e(3)
        if not last:
            nxt_c(kn, PB[1])
        else:
            for q in range(4):
                mass(PB[q], q, "ID4", "NEG")
        for d in range(1, N):
            for i in range(4):
                lo = i * W + OG + GH * (d - 1)
                mm(vw(PA[d - 1], 0, GH), vw("SHP"), vw("SW", lo, lo + GH), i == 0, i == 3)
            if not last:
                nxt_d(kn, d)
            ts(vw(SH, GH * (d - 1), GH * d), vw(PA[d - 1], 0, GH), st, ALU.is_ge, float(8 ** r), ALU.mult)
        send([(N - d, vw(SH, GH * (d - 1), GH * d), vw("HR", GH * (d - 1), GH * d)) for d in range(1, N)], "ah%d" % r)
        for j in range(16):
            for i in range(4):
                lo = i * W + O + j
                mm(vw(PA[3], j, j + 113, 16), vw("SW", lo, lo + E - 15, 16), vw("Z1", 16, 129, 16), i == 0, i == 3)
        ts(vw("hiu"), vw("pt"), 1.0 / 16, ALU.mult, -0.46875, ALU.add)
        ts(vw("shB"), vw("shu", 16, 32), 0.0, ALU.is_equal)
        if not last:
            nxt_e(kn)
        cp(vw("shH"), vw("shu", 16, 32))
        tt(vw("shB"), vw("shB"), vw("shA"), ALU.mult)
        act(vw("xc"), vw("pt"), AF.Relu, bias=2.0, scale=-2.0)
        act(vw("curB"), vw(PA[3], 0, 128), AF.Sign, bias=0.5 - st)
        mm(vw(PA[1], 0, 128), vw("IDB"), vw("xc"), True, False)
        mm(vw(PA[1], 0, 128), vw("curB"), vw("IDB"), False, True)
        act(vw("unl"), vw(PA[1], 0, 128), AF.Sign)
        act(vw("GW", 1, 129), vw("unl"), AF.Relu)
        if last:
            for q in range(4):
                lo = 2 * 512 * (q % 2) + 1 - q // 2
                tt(vw("YS", lo, lo + 1023, 2), ch("YF", q), vw(PB[q]), ALU.add)
            dma("s", lambda: T.ys[:, :], lambda: T.YS[:, :], "sty", [], [vw("YS")])
        if not last:
            mutual_gather(0, 1)
            mutual_conv(PB[0])
        elif r:
            tt(vw("tmp"), vw("MV", 1, 129), vw("dP"), ALU.mult)
            tt(vw("P2"), vw("P2"), vw("tmp"), ALU.add)
        act(vw("EQ", 0, H), (vw("GW"), lists("hiu", 0)))
        conv(vw(PA[0], 0, 64), "ZP", "EQ", 0, 64)
        act(vw("EQ", H, E), (vw("GW"), lists("hiu", 1)))
        act(vw("u0"), vw("GW", 1, 129), AF.Identity, bias=float(8 ** r), scale=-float(8 ** r))
        tt(vw("shB"), vw("shB"), vw("shH"), ALU.add)
        tt(vw("R1"), vw("HR", 0, GH), vw("HR", GH, 2 * GH), ALU.add, waits=[("ah%d" % r, arrivals())])
        cp(vw("shu", 64, 80), vw("shB"))
        tt((vw("RW"), vw("shu", 0, 16)), vw("R1"), vw("HR", 2 * GH, 3 * GH), ALU.add)
        conv(vw(PA[2], 0, 128), "Z1", "RW", O, 128, first=True, last=False)
        tt((vw("RX"), vw("shu", 64, 80)), vw("R1"), vw("HR", 2 * GH, 3 * GH), ALU.add)
        conv(vw(PA[0], 64, 128), "ZP", "EQ", H, 64)
        conv(vw(PA[2], 0, 128), "Z1", "RX", O, 128, first=False, last=True)
        if r and not last:
            tt(vw("tmp"), vw("MV", 1, 129), vw("dP"), ALU.mult)
        if not last:
            tt(vw("lI"), vw(PB[0], 0, 128), vw("P2n%d" % kn), ALU.mult)
        if r and not last:
            tt(vw("P2"), vw("P2"), vw("tmp"), ALU.add)
        if not last:
            ts(vw("lI"), vw("lI"), 15, ALU.arith_shift_right, 1, ALU.bitwise_and)
        tt(vw("tI"), vw(PA[0], 0, 128), vw("P2"), ALU.mult)
        if not last:
            tt(vw("P2q"), vw("lI"), vw("P2n%d" % kn), ALU.mult)
        ts(vw("bitI"), vw("tI"), 15 - 3 * r, ALU.arith_shift_right, 8 ** r, ALU.bitwise_and)
        tt(vw("u0"), vw("u0"), vw("bitI"), ALU.subtract)
        tt(vw("MV", 1, 129), vw(PA[2], 0, 128), vw("u0"), ALU.is_ge)
        if not last:
            look("MV", "hin", PA[1])
            ts(vw("nm"), vw("MV", 1, 129), -1.0, ALU.mult, 1.0, ALU.add)
            tt(vw("P2m"), vw("P2q"), vw("MV", 1, 129), ALU.mult)
            tt(vw("stayb"), vw("nm"), vw("bF"), ALU.mult)
            bit(PA[1], vw("P2m"))
            tt(vw("tmp"), vw("bitI"), vw("bn%d" % kn), ALU.mult)
            tt(vw("pt"), vw("tmp"), vw("stayb"), ALU.add)
            cp(vw("ptu"), vw("pt"))
        else:
            tt(vw("xc"), vw("MV", 1, 129), vw("dc"), ALU.mult)
            for par in range(2):
                n = 0
                for x in ("cB", "xc"):
                    for s in range(2):
                        k = 2 * s + par
                        mm(vw(PB[par], 0, 64), vw("FI", 128 * k, 128 * k + 128), vw(x, 64 * s, 64 * s + 64), n == 0, n == 3)
                        n += 1
            cp(vw("ycs", 0, 127, 2), vw(PB[0], 0, 64))
            act(vw("ycs", 1, 128, 2), vw(PB[1], 0, 64))
            dma("s", lambda: T.yc[:, :], lambda: T.ycs[:, :], "stc", [], [vw("ycs")])

    def meet(a, b):
        return a[0] == b[0] and (a[0][0] == "P" and a[0][1] in "AB" and len(a[0]) == 3 or (a[1] < b[2] and b[1] < a[2]))

    def psum(v):
        return SCRATCH[v[0]][0] == "psum"

    hist = {}
    deps, clock, known = [], [], {}
    for n, o in enumerate(ops):
        dep = set()
        isdma = o["dma"] is not None
        for v, w in [(v, False) for v in o["rd"]] + [(v, True) for v in o["wr"]]:
            for m, u, uw in hist.get(v[0], []):
                p = ops[m]
                if not meet(u, v):
                    continue
                same = p["q"] == o["q"] and p["dma"] is None and not isdma
                exact = u[1] < v[2] and v[1] < u[2]
                if same:
                    if o["q"] != "p" and exact and (uw or w):
                        dep.add(m)
                elif w or uw or psum(v):
                    if p["dma"] != "remote" and not (isdma and p["dma"] == o["dma"]):
                        dep.add(m)
        for v in o["wr"]:
            if v[3] == 1:
                hist[v[0]] = [x for x in hist.get(v[0], []) if not (v[1] <= x[1][1] and x[1][2] <= v[2] and not psum(v))]
            hist.setdefault(v[0], []).append((n, v, True))
        for v in o["rd"]:
            hist.setdefault(v[0], []).append((n, v, False))
        best = {}
        for m in dep:
            key = ops[m]["dma"] or ops[m]["q"]
            best[key] = max(best.get(key, -1), m)
        kn_ = known.setdefault(o["q"], {})
        for key in sorted(best, key=lambda x: -best[x]):
            m = best[key]
            if kn_.get(key, -1) >= m:
                del best[key]
                continue
            kn_[key] = m
            for x, y in clock[m].items():
                kn_[x] = max(kn_.get(x, -1), y)
        clock.append(dict(kn_))
        deps.append(best)
    need = set()
    for n, best in enumerate(deps):
        need |= set(best.values())
    for q in ENG_SEM:
        need.add(max(n for n, o in enumerate(ops) if o["q"] == q and o["dma"] is None))
    total = {}
    for o in ops:
        if o["dma"] not in (None, "remote"):
            total[o["dma"]] = total.get(o["dma"], 0) + 16
    count, mark, seen = {}, {}, {}

    def wait(q, sem, v):
        if seen.get((q, sem), 0) < v:
            Q[q].wait_ge(T.sem[sem], v)
            seen[(q, sem)] = v

    for n, o in enumerate(ops):
        for key, m in deps[n].items():
            if ops[m]["dma"]:
                wait(o["q"], key, total[key])
            else:
                wait(o["q"], ENG_SEM[key], mark[m])
        for sem, v in o["waits"]:
            wait(o["q"], sem, v)
        ins = o["fn"]()
        if o["dma"] is None:
            if n in need:
                count[o["q"]] = count.get(o["q"], 0) + 1
                mark[n] = count[o["q"]]
                ins.then_inc(T.sem[ENG_SEM[o["q"]]], 1)
        elif o["dma"] != "remote":
            ins.then_inc(T.sem[o["dma"]], 16)
    for q in ENG_SEM:
        wait("g", ENG_SEM[q], count[q])
    for sem in total:
        wait("g", sem, total[sem])
    wait("g", "sent", nsent[0])
